import numpy as np
import ml_dtypes


def mxq(x, axis, fmt="e4m3"):
    dtype, down = {"e4m3": (ml_dtypes.float8_e4m3fn, 7), "e5m2": (ml_dtypes.float8_e5m2, 14)}[fmt]
    v = np.moveaxis(np.asarray(x, np.float32).astype(ml_dtypes.bfloat16).astype(np.float64), axis, -1)
    blocks = v.reshape(v.shape[:-1] + (-1, 32))
    amax = np.abs(blocks).max(-1, keepdims=True)
    byte = np.maximum(np.where(amax > 0, np.frexp(amax)[1] - 1 + 127, 0) - down, 1)
    scale = np.exp2(byte - 127.0)
    codes = (blocks / scale).astype(np.float32).astype(dtype).astype(np.float64)
    return np.moveaxis((codes * scale).reshape(v.shape), -1, axis)


WIDE = False


def mx_kscale(k):
    if not WIDE:
        return np.ones(k)
    levels = np.array([24, -24, 12, -12, 0])
    if k % 512:
        return np.exp2(np.random.permutation(np.resize(levels, k // 32))).repeat(32)
    a = np.empty((k // 512, 16))
    for p in range(k // 512):
        a[p, :8] = np.random.permutation(np.resize(levels, 8))
        for g in range(8):
            far = levels[np.abs(levels - a[p, g]) >= 10]
            a[p, g + 8] = far[np.random.randint(len(far))]
    return np.exp2(a.ravel()).repeat(32)


def f64(x):
    return np.asarray(x).astype(np.float64)


def gelu(f):
    return 0.5 * f * (1.0 + np.tanh(np.sqrt(2.0 / np.pi) * (f + 0.044715 * f**3)))


K, J, N, T = 1024, 1024, 512, 1024


def setup_inputs():
    n = np.random.standard_normal
    u = mx_kscale(J)[:, None]
    s = mx_kscale(K)[:, None]
    return {
        "x": (n((K, T)) * s).astype(np.float32),
        "w": (n((K, J)) / np.sqrt(K) / s * 0.4).astype(np.float32),
        "cw": (np.random.uniform(0.5, 2.0, J) * u[:, 0]).astype(np.float32),
        "cb": (0.3 * n(J)).astype(np.float32),
        "v": (n((J, N)) / np.sqrt(J) / u).astype(np.float32),
        "b": (0.3 * n(N)).astype(np.float32),
    }


def reference(x, w, cw, cb, v, b):
    x_ = mxq(f64(x), 0, "e4m3")
    w_ = mxq(f64(w), 0, "e4m3")
    d = w_.T @ x_
    h = f64(cw)[:, None] * np.maximum(d + f64(cb)[:, None], 0.0)
    h_ = mxq(h, 0, "e4m3")
    v_ = mxq(f64(v), 0, "e4m3")
    y = v_.T @ h_
    return gelu(y + f64(b)[:, None])

@@ -1,0 +1,298 @@
+from contextlib import ExitStack
+
+import concourse.mybir as mybir
+
+K, J, N, T = 1024, 1024, 512, 1024
+FLOPS = 2 * K * J * T + 2 * J * N * T
+
+F32 = mybir.dt.float32
+BF16 = mybir.dt.bfloat16
+U32 = mybir.dt.uint32
+U8 = mybir.dt.uint8
+FP8X4 = mybir.dt.float8_e4m3fn_x4
+ALU = mybir.AluOpType
+ACT = mybir.ActivationFunctionType
+
+P = 128
+PACK = 4
+PASS = P * PACK
+RUN = 4
+W = 512
+
+
+TCH = [256, 256, 256, 256]
+ORDER = ["w0", "x0", "x1", "w1", "x2", "v0", "x3", "v1"]
+VW = 256
+MANUAL = True
+PLAN = ""
+
+
+def tile_mix_kern_arc_gelu_kernel(tc, x, w, cw, cb, v, b, out):
+    nc = tc.nc
+    with ExitStack() as ctx:
+        keep = ctx.enter_context(tc.tile_pool(name="keep", bufs=1))
+        psum = ctx.enter_context(tc.psum_pool(name="psum", bufs=1))
+        if MANUAL:
+            ctx.enter_context(tc.manual_schedule())
+
+        def sb(name, shape, dtype):
+            return keep.tile(shape, dtype, name=name, align_bytes=64)
+
+        def copy_on(engine, dst, src):
+            if engine == "V":
+                nc.vector.tensor_copy(out=dst, in_=src)
+            else:
+                nc.scalar.copy(out=dst, in_=src)
+
+        def load(name, rows):
+            raw = sb(name, [P, PACK, rows.shape[1]], F32)
+            nc.sync.dma_start(out=raw[:], in_=rows.rearrange("(p s) c -> p s c", s=PACK))
+            return raw
+
+        def interleave(engine, grouped, raw, lo, hi):
+            if hi > lo:
+                dst = grouped[:, PACK * lo : PACK * hi].rearrange("p (c i s) -> p c s i", i=RUN, s=PACK)
+                src = raw[:, :, lo:hi].rearrange("p s (c i) -> p c s i", i=RUN)
+                copy_on(engine, dst, src)
+
+        def interleave_permuted(engine, grouped, raw, lo, hi):
+            if hi > lo:
+                dst = grouped[:].rearrange("p (u m s) -> p m s u", u=PACK, s=PACK)[:, lo // PACK : hi // PACK]
+                src = raw[:, :, lo:hi].rearrange("p s (m u) -> p m s u", u=PACK)
+                copy_on(engine, dst, src)
+
+        def quantize(name, grouped):
+            width = grouped.shape[1] // PACK
+            codes = sb(name + "_codes", [P, width], U32)
+            scales = sb(name + "_scales", [P, width], U8)
+            nc.vector.quantize_mx(out=codes[:].bitcast(FP8X4), scales=scales[:], in_=grouped[:])
+            return codes, scales
+
+        def mx_pass(acc, stationary, cols, moving, first, last):
+            nc.tensor.matmul_mx(
+                out=acc, lhsT=stationary[0][:, cols].bitcast(FP8X4), lhsT_scale=stationary[1][:, cols],
+                rhs=moving[0][:].bitcast(FP8X4), rhs_scale=moving[1][:], start=first, stop=last,
+            )
+
+
+        cw_sb = sb("cw_sb", [P, 2, PACK], F32)
+        cb_sb = sb("cb_sb", [P, 2, PACK], F32)
+        b_sb = sb("b_sb", [P, PACK], F32)
+        nc.scalar.dma_start(out=cw_sb[:], in_=cw.rearrange("(g p s) -> p g s", p=P, s=PACK))
+        nc.scalar.dma_start(out=cb_sb[:], in_=cb.rearrange("(g p s) -> p g s", p=P, s=PACK))
+        with nc.allow_non_contiguous_dma(reason="one bias value to a partition"):
+            nc.scalar.dma_start(out=b_sb[:], in_=b.rearrange("(q p) -> p q", p=P))
+        starts = [sum(TCH[:i]) for i in range(len(TCH) + 1)]
+        raw = {}
+        for n, item in enumerate(ORDER):
+            kind, c = item[0], int(item[1])
+            for g in range(2):
+                rows = slice(g * PASS, (g + 1) * PASS)
+                if kind == "w":
+                    src = w[rows, c * W : (c + 1) * W]
+                elif kind == "x":
+                    src = x[rows, starts[c] : starts[c + 1]]
+                else:
+                    src = v[rows, c * VW : (c + 1) * VW]
+                raw[kind, c, g] = load("%s_raw%d%d" % (kind, c, g), src)
+
+        warm = sb("warm", [P, 1], F32)
+        warm2 = sb("warm2", [P, 1], F32)
+        nc.vector.memset(warm[:], 0.0)
+        nc.scalar.activation(out=warm2[:], in_=warm[:], func=ACT.Gelu_apprx_tanh)
+
+        sign = sb("sign", [P, 2, PACK], F32)
+        sign01 = sb("sign01", [P, 2, PACK], F32)
+        gain = sb("gain", [P, 2, PACK], F32)
+        shift = sb("shift", [P, 2, PACK], F32)
+
+        def constants():
+            nc.vector.tensor_scalar(out=sign01[:], in0=cw_sb[:], scalar1=0.0, scalar2=2.0, op0=ALU.is_ge, op1=ALU.mult)
+            nc.vector.tensor_scalar(out=sign[:], in0=sign01[:], scalar1=-1.0, scalar2=None, op0=ALU.add)
+            nc.vector.tensor_tensor(out=gain[:], in0=cw_sb[:], in1=sign[:], op=ALU.mult)
+            nc.vector.tensor_tensor(out=shift[:], in0=cb_sb[:], in1=gain[:], op=ALU.mult)
+
+
+        x_codes = [sb("x_codes%d" % g, [P, T], U32) for g in range(2)]
+        x_scales = [sb("x_scales%d" % g, [P, T], U8) for g in range(2)]
+        h_codes = [sb("h_codes%d" % g, [P, T], U32) for g in range(2)]
+        h_scales = [sb("h_scales%d" % g, [P, T], U8) for g in range(2)]
+        grp, wq, vq, accs, rows, res = {}, {}, {}, {}, {}, {}
+
+        def copy_in(kind, c, g, engine, lo, hi):
+            r = raw[kind, c, g]
+            if (kind, c, g) not in grp:
+                grp[kind, c, g] = sb("%s_grp%d%d" % (kind, c, g), [P, PACK * r.shape[2]], BF16)
+            fn = interleave if kind == "x" else interleave_permuted
+            fn(engine, grp[kind, c, g], r, lo, hi)
+
+        def quant_in(kind, c, g):
+            if kind == "w":
+                wq[c, g] = quantize("w%d%d" % (c, g), grp[kind, c, g])
+            else:
+                cols = slice(starts[c], starts[c + 1])
+                nc.vector.quantize_mx(out=x_codes[g][:, cols].bitcast(FP8X4), scales=x_scales[g][:, cols], in_=grp[kind, c, g][:])
+
+        def stage1(jg, lo, hi, bank0, passes):
+            for u in range(PACK):
+                if passes[0] == 0:
+                    accs[jg, lo, u] = psum.tile([P, W], F32, name="d%d_%d_%d" % (jg, lo, u), tag="bank%d" % (bank0 + u))
+                for g in passes:
+                    nc.tensor.matmul_mx(
+                        out=accs[jg, lo, u][:, : hi - lo], lhsT=wq[jg, g][0][:, u * P : (u + 1) * P].bitcast(FP8X4),
+                        lhsT_scale=wq[jg, g][1][:, u * P : (u + 1) * P],
+                        rhs=x_codes[g][:, lo:hi].bitcast(FP8X4), rhs_scale=x_scales[g][:, lo:hi], start=g == 0, stop=g == 1,
+                    )
+
+        def evac(jg, lo, hi, engines):
+            for u in range(PACK):
+                if (jg, lo) not in rows:
+                    rows[jg, lo] = sb("h_rows%d_%d" % (jg, lo), [P, PACK, hi - lo], BF16)
+                src = accs[jg, lo, u][:, : hi - lo]
+                if engines[u] == "V":
+                    nc.vector.tensor_scalar(out=rows[jg, lo][:, u, :], in0=src, scalar1=gain[:, jg, u : u + 1],
+                                            scalar2=shift[:, jg, u : u + 1], op0=ALU.mult, op1=ALU.add)
+                elif engines[u] == "S":
+                    nc.scalar.activation(out=rows[jg, lo][:, u, :], in_=src, func=ACT.Identity,
+                                         bias=shift[:, jg, u : u + 1], scale=gain[:, jg, u : u + 1])
+
+        def h_weave(jg, lo):
+            width = rows[jg, lo].shape[2]
+            grp["h", jg, lo] = sb("h_grp%d_%d" % (jg, lo), [P, PACK * width], BF16)
+            dst = grp["h", jg, lo][:].rearrange("p (c i s) -> p c s i", i=RUN, s=PACK)
+            src = rows[jg, lo][:].rearrange("p s (c i) -> p c s i", i=RUN)
+            nc.vector.tensor_scalar(out=dst, in0=src, scalar1=0.0, scalar2=None, op0=ALU.max)
+
+        def h_quant(jg, lo):
+            cols = slice(lo, lo + rows[jg, lo].shape[2])
+            nc.vector.quantize_mx(out=h_codes[jg][:, cols].bitcast(FP8X4), scales=h_scales[jg][:, cols], in_=grp["h", jg, lo][:])
+
+        signs = sb("signs", [P, 2, PACK * VW], BF16)
+
+        def spread_signs():
+            for g in range(2):
+                nc.scalar.copy(out=signs[:, g].rearrange("p (c s) -> p c s", s=PACK),
+                               in_=sign[:, g, :].unsqueeze(1).to_broadcast([P, VW, PACK]))
+
+        def v_weave(c, g, engine):
+            grp["v", c, g] = sb("v_grp%d%d" % (c, g), [P, PACK * VW], BF16)
+            interleave(engine, grp["v", c, g], raw["v", c, g], 0, VW)
+
+        def v_sign(c, g):
+            grp["vs", c, g] = sb("v_sgn%d%d" % (c, g), [P, PACK * VW], BF16)
+            nc.vector.tensor_tensor(out=grp["vs", c, g][:], in0=grp["v", c, g][:], in1=signs[:, g], op=ALU.mult)
+
+        def v_quant(c, g):
+            vq[c, g] = quantize("v%d%d" % (c, g), grp["vs", c, g])
+
+        def stage2(nq, lo, hi, bank):
+            accs["y", nq, lo] = psum.tile([P, W], F32, name="y%d_%d" % (nq, lo), tag="bank%d" % bank)
+            c, off = divmod(nq * P, VW)
+            for g in range(2):
+                nc.tensor.matmul_mx(
+                    out=accs["y", nq, lo][:, : hi - lo], lhsT=vq[c, g][0][:, off : off + P].bitcast(FP8X4),
+                    lhsT_scale=vq[c, g][1][:, off : off + P],
+                    rhs=h_codes[g][:, lo:hi].bitcast(FP8X4), rhs_scale=h_scales[g][:, lo:hi], start=g == 0, stop=g == 1,
+                )
+
+        def finish(nq, lo, hi):
+            res[nq, lo] = sb("y_sb%d_%d" % (nq, lo), [P, hi - lo], F32)
+            nc.scalar.activation(out=res[nq, lo][:], in_=accs["y", nq, lo][:, : hi - lo], func=ACT.Gelu_apprx_tanh, bias=b_sb[:, nq : nq + 1])
+            nc.sync.dma_start(out=out[nq * P : (nq + 1) * P, lo:hi], in_=res[nq, lo][:])
+
+
+        constants()
+        spread_signs()
+        copy_in("w", 0, 0, "V", 0, 512)
+        quant_in("w", 0, 0)
+        copy_in("w", 0, 1, "S", 336, 512)
+        copy_in("w", 0, 1, "V", 0, 336)
+        quant_in("w", 0, 1)
+        copy_in("x", 0, 0, "S", 128, 256)
+        copy_in("x", 0, 0, "V", 0, 128)
+        copy_in("x", 0, 1, "S", 176, 256)
+        quant_in("x", 0, 0)
+        stage1(0, 0, 256, 0, [0])
+        copy_in("x", 0, 1, "V", 0, 176)
+        quant_in("x", 0, 1)
+        stage1(0, 0, 256, 0, [1])
+        copy_in("x", 1, 0, "V", 0, 256)
+        evac(0, 0, 256, "SSSS")
+        quant_in("x", 1, 0)
+        stage1(0, 256, 512, 4, [0])
+        copy_in("x", 1, 1, "V", 0, 256)
+        quant_in("x", 1, 1)
+        stage1(0, 256, 512, 4, [1])
+        h_weave(0, 0)
+        evac(0, 256, 512, "SSSS")
+        h_quant(0, 0)
+        copy_in("w", 1, 0, "S", 384, 512)
+        copy_in("w", 1, 0, "V", 0, 384)
+        h_weave(0, 256)
+        quant_in("w", 1, 0)
+        stage1(1, 0, 512, 0, [0])
+        h_quant(0, 256)
+        copy_in("w", 1, 1, "S", 336, 512)
+        copy_in("w", 1, 1, "V", 0, 336)
+        quant_in("w", 1, 1)
+        stage1(1, 0, 512, 0, [1])
+
+        copy_in("x", 2, 0, "S", 0, 256)
+        evac(1, 0, 512, "SSSS")
+        copy_in("x", 2, 1, "V", 0, 256)
+        quant_in("x", 2, 0)
+        quant_in("x", 2, 1)
+        stage1(0, 512, 768, 4, [0, 1])
+        v_weave(0, 0, "V")
+        evac(0, 512, 768, "SSSS")
+        stage1(1, 512, 768, 0, [0, 1])
+        v_sign(0, 0)
+        v_weave(0, 1, "V")
+        v_quant(0, 0)
+        v_sign(0, 1)
+        evac(1, 512, 768, "SSSS")
+        h_weave(1, 0)
+        v_quant(0, 1)
+        h_quant(1, 0)
+        stage2(0, 0, 512, 4)
+        stage2(1, 0, 512, 5)
+        copy_in("x", 3, 0, "V", 0, 256)
+        copy_in("x", 3, 1, "V", 0, 256)
+        quant_in("x", 3, 0)
+        quant_in("x", 3, 1)
+        v_weave(1, 0, "S")
+        finish(0, 0, 512)
+        finish(1, 0, 512)
+        stage1(0, 768, 1024, 0, [0, 1])
+        stage1(1, 768, 1024, 4, [0, 1])
+        h_weave(0, 512)
+        h_weave(1, 512)
+        h_quant(0, 512)
+        h_quant(1, 512)
+        evac(0, 768, 1024, "SSSS")
+        stage2(0, 512, 768, 0)
+        stage2(1, 512, 768, 1)
+        v_weave(1, 1, "V")
+        v_sign(1, 0)
+        v_sign(1, 1)
+        v_quant(1, 0)
+        v_quant(1, 1)
+        evac(1, 768, 1024, "SSSS")
+        stage2(2, 0, 512, 2)
+        stage2(3, 0, 512, 3)
+        stage2(2, 512, 768, 4)
+        stage2(3, 512, 768, 5)
+        finish(0, 512, 768)
+        finish(1, 512, 768)
+        finish(2, 0, 512)
+        finish(3, 0, 512)
+        finish(2, 512, 768)
+        finish(3, 512, 768)
+        h_weave(0, 768)
+        h_weave(1, 768)
+        h_quant(0, 768)
+        h_quant(1, 768)
+        for nq in range(4):
+            stage2(nq, 768, 1024, [6, 7, 0, 1][nq])
+        for nq in range(4):
+            finish(nq, 768, 1024)

@@ -1,6 +1,7 @@
 from contextlib import ExitStack
 
 import concourse.mybir as mybir
+from concourse.masks import make_identity
 
 K, J, N, T = 1024, 1024, 512, 1024
 FLOPS = 2 * K * J * T + 2 * J * N * T
@@ -75,13 +76,12 @@ def tile_mix_kern_arc_gelu_kernel(tc, x, w, cw, cb, v, b, out):
             )
 
 
-        cw_sb = sb("cw_sb", [P, 2, PACK], F32)
         cb_sb = sb("cb_sb", [P, 2, PACK], F32)
         b_sb = sb("b_sb", [P, PACK], F32)
-        nc.scalar.dma_start(out=cw_sb[:], in_=cw.rearrange("(g p s) -> p g s", p=P, s=PACK))
-        nc.scalar.dma_start(out=cb_sb[:], in_=cb.rearrange("(g p s) -> p g s", p=P, s=PACK))
-        with nc.allow_non_contiguous_dma(reason="one bias value to a partition"):
-            nc.scalar.dma_start(out=b_sb[:], in_=b.rearrange("(q p) -> p q", p=P))
+        stage = sb("stage", [P, PASS], F32)
+        ident = sb("ident", [P, P], F32)
+        nc.vector.memset(stage[:], 0.0)
+        make_identity(nc, ident[:])
         starts = [sum(TCH[:i]) for i in range(len(TCH) + 1)]
         raw = {}
         for n, item in enumerate(ORDER):
@@ -95,6 +95,10 @@ def tile_mix_kern_arc_gelu_kernel(tc, x, w, cw, cb, v, b, out):
                 else:
                     src = v[rows, c * VW : (c + 1) * VW]
                 raw[kind, c, g] = load("%s_raw%d%d" % (kind, c, g), src)
+                if n == 0 and g == 0:
+                    nc.sync.dma_start(out=stage[0:2, :], in_=cw.rearrange("(g c) -> g c", g=2))
+                    nc.sync.dma_start(out=stage[2:4, :], in_=cb.rearrange("(g c) -> g c", g=2))
+                    nc.sync.dma_start(out=stage[4:8, 0:P], in_=b.rearrange("(q p) -> q p", p=P))
 
         warm = sb("warm", [P, 1], F32)
         warm2 = sb("warm2", [P, 1], F32)
@@ -102,16 +106,22 @@ def tile_mix_kern_arc_gelu_kernel(tc, x, w, cw, cb, v, b, out):
         nc.scalar.activation(out=warm2[:], in_=warm[:], func=ACT.Gelu_apprx_tanh)
 
         sign = sb("sign", [P, 2, PACK], F32)
-        sign01 = sb("sign01", [P, 2, PACK], F32)
         gain = sb("gain", [P, 2, PACK], F32)
         shift = sb("shift", [P, 2, PACK], F32)
 
         def constants():
-            nc.vector.tensor_scalar(out=sign01[:], in0=cw_sb[:], scalar1=0.0, scalar2=2.0, op0=ALU.is_ge, op1=ALU.mult)
-            nc.vector.tensor_scalar(out=sign[:], in0=sign01[:], scalar1=-1.0, scalar2=None, op0=ALU.add)
-            nc.vector.tensor_tensor(out=gain[:], in0=cw_sb[:], in1=sign[:], op=ALU.mult)
-            nc.vector.tensor_tensor(out=shift[:], in0=cb_sb[:], in1=gain[:], op=ALU.mult)
+            turned = psum.tile([P, PACK, P], F32, name="turned", tag="bank6")
+            turned_b = psum.tile([P, P], F32, name="turned_b", tag="bank7")
+            for slot in range(PACK):
+                nc.tensor.transpose(turned[:, slot, :], stage[:, slot::PACK], ident[:])
+            nc.tensor.transpose(turned_b[:], stage[:, 0:P], ident[:])
+            nc.scalar.activation(out=gain[:], in_=turned[:, :, 0:2].rearrange("p s g -> p g s"), func=ACT.Abs)
+            nc.scalar.activation(out=sign[:], in_=turned[:, :, 0:2].rearrange("p s g -> p g s"), func=ACT.Sign)
+            nc.scalar.copy(out=cb_sb[:], in_=turned[:, :, 2:4].rearrange("p s g -> p g s"))
+            nc.scalar.copy(out=b_sb[:], in_=turned_b[:, 4:8])
 
+        def scaled_offsets():
+            nc.vector.tensor_tensor(out=shift[:], in0=cb_sb[:], in1=gain[:], op=ALU.mult)
 
         x_codes = [sb("x_codes%d" % g, [P, T], U32) for g in range(2)]
         x_scales = [sb("x_scales%d" % g, [P, T], U8) for g in range(2)]
@@ -169,10 +179,9 @@ def tile_mix_kern_arc_gelu_kernel(tc, x, w, cw, cb, v, b, out):
 
         signs = sb("signs", [P, 2, PACK * VW], BF16)
 
-        def spread_signs():
-            for g in range(2):
-                nc.scalar.copy(out=signs[:, g].rearrange("p (c s) -> p c s", s=PACK),
-                               in_=sign[:, g, :].unsqueeze(1).to_broadcast([P, VW, PACK]))
+        def spread_signs(g):
+            nc.scalar.copy(out=signs[:, g].rearrange("p (c s) -> p c s", s=PACK),
+                           in_=sign[:, g, :].unsqueeze(1).to_broadcast([P, VW, PACK]))
 
         def v_weave(c, g, engine):
             grp["v", c, g] = sb("v_grp%d%d" % (c, g), [P, PACK * VW], BF16)
@@ -201,16 +210,18 @@ def tile_mix_kern_arc_gelu_kernel(tc, x, w, cw, cb, v, b, out):
             nc.sync.dma_start(out=out[nq * P : (nq + 1) * P, lo:hi], in_=res[nq, lo][:])
 
 
-        constants()
-        spread_signs()
         copy_in("w", 0, 0, "V", 0, 512)
         quant_in("w", 0, 0)
         copy_in("w", 0, 1, "S", 336, 512)
+        constants()
         copy_in("w", 0, 1, "V", 0, 336)
         quant_in("w", 0, 1)
         copy_in("x", 0, 0, "S", 128, 256)
         copy_in("x", 0, 0, "V", 0, 128)
+        scaled_offsets()
         copy_in("x", 0, 1, "S", 176, 256)
+        spread_signs(0)
+        spread_signs(1)
         quant_in("x", 0, 0)
         stage1(0, 0, 256, 0, [0])
         copy_in("x", 0, 1, "V", 0, 176)

@@ -18,14 +18,7 @@ P = 128
 PACK = 4
 PASS = P * PACK
 RUN = 4
-W = 512
-
-
-TCH = [256, 256, 256, 256]
-ORDER = ["w0", "x0", "x1", "w1", "x2", "v0", "x3", "v1"]
-VW = 256
-MANUAL = True
-PLAN = ""
+BANK = 512
 
 
 def tile_mix_kern_arc_gelu_kernel(tc, x, w, cw, cb, v, b, out):
@@ -33,83 +26,136 @@ def tile_mix_kern_arc_gelu_kernel(tc, x, w, cw, cb, v, b, out):
     with ExitStack() as ctx:
         keep = ctx.enter_context(tc.tile_pool(name="keep", bufs=1))
         psum = ctx.enter_context(tc.psum_pool(name="psum", bufs=1))
-        if MANUAL:
-            ctx.enter_context(tc.manual_schedule())
+        ctx.enter_context(tc.manual_schedule())
 
         def sb(name, shape, dtype):
             return keep.tile(shape, dtype, name=name, align_bytes=64)
 
-        def copy_on(engine, dst, src):
-            if engine == "V":
-                nc.vector.tensor_copy(out=dst, in_=src)
+        hbm = {"w": w, "x": x, "v": v}
+        raw, woven, accs, rows = {}, {}, {}, {}
+        codes = {(kind, g): sb("%s_codes%d" % (kind, g), [P, width], U32)
+                 for kind, width in (("w", J), ("x", T), ("v", N), ("h", T)) for g in range(2)}
+        scales = {(kind, g): sb("%s_scales%d" % (kind, g), [P, width], U8)
+                  for kind, width in (("w", J), ("x", T), ("v", N), ("h", T)) for g in range(2)}
+
+        def load(kind, g, lo, hi):
+            tile = sb("%s_raw%d_%d" % (kind, g, lo), [P, PACK, hi - lo], F32)
+            nc.sync.dma_start(out=tile[:], in_=hbm[kind][g * PASS : (g + 1) * PASS, lo:hi].rearrange("(p s) c -> p s c", s=PACK))
+            raw.setdefault((kind, g), []).append((lo, hi, tile[:]))
+
+        def find(table, key, lo, hi):
+            for a, z, ap in table[key]:
+                if a <= lo and hi <= z:
+                    return a, ap
+            raise ValueError("no tile holds these columns")
+
+        def block(kind, g, lo, hi):
+            woven.setdefault((kind, g), []).append((lo, hi, sb("%s_woven%d_%d" % (kind, g, lo), [P, PACK * (hi - lo)], BF16)[:]))
+
+        def weave(engine, kind, g, lo, hi):
+            a, src = find(rows if (kind, g) in rows else raw, (kind, g), lo, hi)
+            src = src[:, :, lo - a : hi - a]
+            a, dst = find(woven, (kind, g), lo, hi)
+            if kind == "w":
+                dst = dst.rearrange("p (u m s) -> p m s u", u=PACK, s=PACK)[:, (lo - a) // PACK : (hi - a) // PACK]
+                src = src.rearrange("p s (m u) -> p m s u", u=PACK)
             else:
+                dst = dst[:, PACK * (lo - a) : PACK * (hi - a)].rearrange("p (c i s) -> p c s i", i=RUN, s=PACK)
+                src = src.rearrange("p s (c i) -> p c s i", i=RUN)
+            if engine == "S":
                 nc.scalar.copy(out=dst, in_=src)
+            elif kind == "h":
+                nc.vector.tensor_scalar(out=dst, in0=src, scalar1=0.0, scalar2=None, op0=ALU.max)
+            else:
+                nc.vector.tensor_copy(out=dst, in_=src)
 
-        def load(name, rows):
-            raw = sb(name, [P, PACK, rows.shape[1]], F32)
-            nc.sync.dma_start(out=raw[:], in_=rows.rearrange("(p s) c -> p s c", s=PACK))
-            return raw
+        def shared_weave(kind, g, lo, cut, hi):
+            weave("S", kind, g, cut, hi)
+            weave("V", kind, g, lo, cut)
 
-        def interleave(engine, grouped, raw, lo, hi):
-            if hi > lo:
-                dst = grouped[:, PACK * lo : PACK * hi].rearrange("p (c i s) -> p c s i", i=RUN, s=PACK)
-                src = raw[:, :, lo:hi].rearrange("p s (c i) -> p c s i", i=RUN)
-                copy_on(engine, dst, src)
+        def quantize(kind, g, lo, hi):
+            a, src = find(woven, (kind, g), lo, hi)
+            nc.vector.quantize_mx(out=codes[kind, g][:, lo:hi].bitcast(FP8X4), scales=scales[kind, g][:, lo:hi],
+                                  in_=src[:, PACK * (lo - a) : PACK * (hi - a)])
 
-        def interleave_permuted(engine, grouped, raw, lo, hi):
-            if hi > lo:
-                dst = grouped[:].rearrange("p (u m s) -> p m s u", u=PACK, s=PACK)[:, lo // PACK : hi // PACK]
-                src = raw[:, :, lo:hi].rearrange("p s (m u) -> p m s u", u=PACK)
-                copy_on(engine, dst, src)
-
-        def quantize(name, grouped):
-            width = grouped.shape[1] // PACK
-            codes = sb(name + "_codes", [P, width], U32)
-            scales = sb(name + "_scales", [P, width], U8)
-            nc.vector.quantize_mx(out=codes[:].bitcast(FP8X4), scales=scales[:], in_=grouped[:])
-            return codes, scales
-
-        def mx_pass(acc, stationary, cols, moving, first, last):
+        def mx_pass(acc, stationary, cols, moving, g, lo, hi, first, last):
             nc.tensor.matmul_mx(
-                out=acc, lhsT=stationary[0][:, cols].bitcast(FP8X4), lhsT_scale=stationary[1][:, cols],
-                rhs=moving[0][:].bitcast(FP8X4), rhs_scale=moving[1][:], start=first, stop=last,
+                out=acc, lhsT=codes[stationary, g][:, cols].bitcast(FP8X4), lhsT_scale=scales[stationary, g][:, cols],
+                rhs=codes[moving, g][:, lo:hi].bitcast(FP8X4), rhs_scale=scales[moving, g][:, lo:hi], start=first, stop=last,
             )
 
+        def product1(jg, lo, hi, banks, passes=(0, 1)):
+            per = PACK // len(banks)
+            for n, bank in enumerate(banks):
+                if passes[0] == 0:
+                    tile = psum.tile([P, per, BANK // per], F32, name="d%d_%d_%d" % (jg, lo, n), tag="bank%d" % bank)
+                    for m in range(per):
+                        accs["d", jg, lo, n * per + m] = tile[:, m, : hi - lo]
+                for g in passes:
+                    for m in range(per):
+                        u = n * per + m
+                        cols = slice(jg * PASS + u * P, jg * PASS + (u + 1) * P)
+                        mx_pass(accs["d", jg, lo, u], "w", cols, "x", g, lo, hi, g == 0 and m == 0, g == 1 and m == per - 1)
+
+        def h_rows(jg, lo, hi):
+            rows.setdefault(("h", jg), []).append((lo, hi, sb("h_rows%d_%d" % (jg, lo), [P, PACK, hi - lo], BF16)[:]))
+
+        def drain(engine, jg, lo, hi, slots):
+            a, dst = find(rows, ("h", jg), lo, hi)
+            for u in slots:
+                src = accs["d", jg, lo, u]
+                if engine == "V":
+                    nc.vector.tensor_scalar(out=dst[:, u, lo - a : hi - a], in0=src, scalar1=gain[:, jg, u : u + 1],
+                                            scalar2=shift[:, jg, u : u + 1], op0=ALU.mult, op1=ALU.add)
+                else:
+                    nc.scalar.activation(out=dst[:, u, lo - a : hi - a], in_=src, func=ACT.Relu,
+                                         bias=shift[:, jg, u : u + 1], scale=gain[:, jg, u : u + 1])
+
+        def v_rows(g, lo, hi):
+            rows.setdefault(("v", g), []).append((lo, hi, sb("v_rows%d_%d" % (g, lo), [P, PACK, hi - lo], BF16)[:]))
+
+        def v_sign(engine, g, lo, hi, slots=range(PACK)):
+            a, src = find(raw, ("v", g), lo, hi)
+            c, dst = find(rows, ("v", g), lo, hi)
+            for s in slots:
+                if engine == "S":
+                    nc.scalar.activation(out=dst[:, s, lo - c : hi - c], in_=src[:, s, lo - a : hi - a], func=ACT.Copy, scale=sign[:, g, s : s + 1])
+                else:
+                    nc.vector.tensor_scalar(out=dst[:, s, lo - c : hi - c], in0=src[:, s, lo - a : hi - a], scalar1=sign[:, g, s : s + 1],
+                                            scalar2=None, op0=ALU.mult)
+
+        def product2(lo, hi, banks, passes=(0, 1), tiles=range(PACK)):
+            per = len(tiles) // len(banks)
+            for n, bank in enumerate(banks):
+                if passes[0] == 0:
+                    tile = psum.tile([P, per, BANK // per], F32, name="y%d_%d" % (lo, tiles[n * per]), tag="bank%d" % bank)
+                    for m in range(per):
+                        accs["y", tiles[n * per + m], lo] = tile[:, m, : hi - lo]
+                for g in passes:
+                    for m in range(per):
+                        q = tiles[n * per + m]
+                        mx_pass(accs["y", q, lo], "v", slice(q * P, (q + 1) * P), "h", g, lo, hi, g == 0 and m == 0, g == 1 and m == per - 1)
+
+        def finish(lo, hi, tiles=range(PACK)):
+            for q in tiles:
+                res = sb("y_sb%d_%d" % (q, lo), [P, hi - lo], F32)
+                nc.scalar.activation(out=res[:], in_=accs["y", q, lo], func=ACT.Gelu_apprx_tanh, bias=b_sb[:, q : q + 1])
+                nc.sync.dma_start(out=out[q * P : (q + 1) * P, lo:hi], in_=res[:])
 
         cb_sb = sb("cb_sb", [P, 2, PACK], F32)
         b_sb = sb("b_sb", [P, PACK], F32)
-        stage = sb("stage", [P, PASS], F32)
-        ident = sb("ident", [P, P], F32)
-        nc.vector.memset(stage[:], 0.0)
-        make_identity(nc, ident[:])
-        starts = [sum(TCH[:i]) for i in range(len(TCH) + 1)]
-        raw = {}
-        for n, item in enumerate(ORDER):
-            kind, c = item[0], int(item[1])
-            for g in range(2):
-                rows = slice(g * PASS, (g + 1) * PASS)
-                if kind == "w":
-                    src = w[rows, c * W : (c + 1) * W]
-                elif kind == "x":
-                    src = x[rows, starts[c] : starts[c + 1]]
-                else:
-                    src = v[rows, c * VW : (c + 1) * VW]
-                raw[kind, c, g] = load("%s_raw%d%d" % (kind, c, g), src)
-                if n == 0 and g == 0:
-                    nc.sync.dma_start(out=stage[0:2, :], in_=cw.rearrange("(g c) -> g c", g=2))
-                    nc.sync.dma_start(out=stage[2:4, :], in_=cb.rearrange("(g c) -> g c", g=2))
-                    nc.sync.dma_start(out=stage[4:8, 0:P], in_=b.rearrange("(q p) -> q p", p=P))
-
-        warm = sb("warm", [P, 1], F32)
-        warm2 = sb("warm2", [P, 1], F32)
-        nc.vector.memset(warm[:], 0.0)
-        nc.scalar.activation(out=warm2[:], in_=warm[:], func=ACT.Gelu_apprx_tanh)
-
         sign = sb("sign", [P, 2, PACK], F32)
         gain = sb("gain", [P, 2, PACK], F32)
         shift = sb("shift", [P, 2, PACK], F32)
+        stage = sb("stage", [P, PASS], F32)
+        ident = sb("ident", [P, P], F32)
 
-        def constants():
+        def load_vectors():
+            nc.sync.dma_start(out=stage[0:2, :], in_=cw.rearrange("(g c) -> g c", g=2))
+            nc.sync.dma_start(out=stage[2:4, :], in_=cb.rearrange("(g c) -> g c", g=2))
+            nc.sync.dma_start(out=stage[4:8, 0:P], in_=b.rearrange("(q p) -> q p", p=P))
+
+        def turn_vectors():
             turned = psum.tile([P, PACK, P], F32, name="turned", tag="bank6")
             turned_b = psum.tile([P, P], F32, name="turned_b", tag="bank7")
             for slot in range(PACK):
@@ -123,187 +169,121 @@ def tile_mix_kern_arc_gelu_kernel(tc, x, w, cw, cb, v, b, out):
         def scaled_offsets():
             nc.vector.tensor_tensor(out=shift[:], in0=cb_sb[:], in1=gain[:], op=ALU.mult)
 
-        x_codes = [sb("x_codes%d" % g, [P, T], U32) for g in range(2)]
-        x_scales = [sb("x_scales%d" % g, [P, T], U8) for g in range(2)]
-        h_codes = [sb("h_codes%d" % g, [P, T], U32) for g in range(2)]
-        h_scales = [sb("h_scales%d" % g, [P, T], U8) for g in range(2)]
-        grp, wq, vq, accs, rows, res = {}, {}, {}, {}, {}, {}
+        def prepare():
+            nc.vector.memset(stage[:], 0.0)
+            make_identity(nc, ident[:])
 
-        def copy_in(kind, c, g, engine, lo, hi):
-            r = raw[kind, c, g]
-            if (kind, c, g) not in grp:
-                grp[kind, c, g] = sb("%s_grp%d%d" % (kind, c, g), [P, PACK * r.shape[2]], BF16)
-            fn = interleave if kind == "x" else interleave_permuted
-            fn(engine, grp[kind, c, g], r, lo, hi)
+        def warm_table():
+            warm2 = sb("warm2", [P, 1], F32)
+            nc.scalar.activation(out=warm2[:], in_=ident[:, 0:1], func=ACT.Gelu_apprx_tanh)
 
-        def quant_in(kind, c, g):
-            if kind == "w":
-                wq[c, g] = quantize("w%d%d" % (c, g), grp[kind, c, g])
-            else:
-                cols = slice(starts[c], starts[c + 1])
-                nc.vector.quantize_mx(out=x_codes[g][:, cols].bitcast(FP8X4), scales=x_scales[g][:, cols], in_=grp[kind, c, g][:])
 
-        def stage1(jg, lo, hi, bank0, passes):
-            for u in range(PACK):
-                if passes[0] == 0:
-                    accs[jg, lo, u] = psum.tile([P, W], F32, name="d%d_%d_%d" % (jg, lo, u), tag="bank%d" % (bank0 + u))
-                for g in passes:
-                    nc.tensor.matmul_mx(
-                        out=accs[jg, lo, u][:, : hi - lo], lhsT=wq[jg, g][0][:, u * P : (u + 1) * P].bitcast(FP8X4),
-                        lhsT_scale=wq[jg, g][1][:, u * P : (u + 1) * P],
-                        rhs=x_codes[g][:, lo:hi].bitcast(FP8X4), rhs_scale=x_scales[g][:, lo:hi], start=g == 0, stop=g == 1,
-                    )
-
-        def evac(jg, lo, hi, engines):
-            for u in range(PACK):
-                if (jg, lo) not in rows:
-                    rows[jg, lo] = sb("h_rows%d_%d" % (jg, lo), [P, PACK, hi - lo], BF16)
-                src = accs[jg, lo, u][:, : hi - lo]
-                if engines[u] == "V":
-                    nc.vector.tensor_scalar(out=rows[jg, lo][:, u, :], in0=src, scalar1=gain[:, jg, u : u + 1],
-                                            scalar2=shift[:, jg, u : u + 1], op0=ALU.mult, op1=ALU.add)
-                elif engines[u] == "S":
-                    nc.scalar.activation(out=rows[jg, lo][:, u, :], in_=src, func=ACT.Identity,
-                                         bias=shift[:, jg, u : u + 1], scale=gain[:, jg, u : u + 1])
-
-        def h_weave(jg, lo):
-            width = rows[jg, lo].shape[2]
-            grp["h", jg, lo] = sb("h_grp%d_%d" % (jg, lo), [P, PACK * width], BF16)
-            dst = grp["h", jg, lo][:].rearrange("p (c i s) -> p c s i", i=RUN, s=PACK)
-            src = rows[jg, lo][:].rearrange("p s (c i) -> p c s i", i=RUN)
-            nc.vector.tensor_scalar(out=dst, in0=src, scalar1=0.0, scalar2=None, op0=ALU.max)
-
-        def h_quant(jg, lo):
-            cols = slice(lo, lo + rows[jg, lo].shape[2])
-            nc.vector.quantize_mx(out=h_codes[jg][:, cols].bitcast(FP8X4), scales=h_scales[jg][:, cols], in_=grp["h", jg, lo][:])
-
-        signs = sb("signs", [P, 2, PACK * VW], BF16)
-
-        def spread_signs(g):
-            nc.scalar.copy(out=signs[:, g].rearrange("p (c s) -> p c s", s=PACK),
-                           in_=sign[:, g, :].unsqueeze(1).to_broadcast([P, VW, PACK]))
-
-        def v_weave(c, g, engine):
-            grp["v", c, g] = sb("v_grp%d%d" % (c, g), [P, PACK * VW], BF16)
-            interleave(engine, grp["v", c, g], raw["v", c, g], 0, VW)
-
-        def v_sign(c, g):
-            grp["vs", c, g] = sb("v_sgn%d%d" % (c, g), [P, PACK * VW], BF16)
-            nc.vector.tensor_tensor(out=grp["vs", c, g][:], in0=grp["v", c, g][:], in1=signs[:, g], op=ALU.mult)
-
-        def v_quant(c, g):
-            vq[c, g] = quantize("v%d%d" % (c, g), grp["vs", c, g])
-
-        def stage2(nq, lo, hi, bank):
-            accs["y", nq, lo] = psum.tile([P, W], F32, name="y%d_%d" % (nq, lo), tag="bank%d" % bank)
-            c, off = divmod(nq * P, VW)
+        prepare()
+        load("w", 0, 0, 1024)
+        load_vectors()
+        a, bb, c, d = [(lo, lo + 256) for lo in range(0, T, 256)]
+        load("x", 0, *a)
+        load("w", 1, 0, 1024)
+        load("x", 1, *a)
+        for lo, hi in (bb, c):
             for g in range(2):
-                nc.tensor.matmul_mx(
-                    out=accs["y", nq, lo][:, : hi - lo], lhsT=vq[c, g][0][:, off : off + P].bitcast(FP8X4),
-                    lhsT_scale=vq[c, g][1][:, off : off + P],
-                    rhs=h_codes[g][:, lo:hi].bitcast(FP8X4), rhs_scale=h_scales[g][:, lo:hi], start=g == 0, stop=g == 1,
-                )
+                load("x", g, lo, hi)
+        for g in range(2):
+            load("v", g, 0, 512)
+        for g in range(2):
+            load("x", g, *d)
+        warm_table()
+        for kind in "xh":
+            for g in range(2):
+                for lo, hi in (a, bb, c, d):
+                    block(kind, g, lo, hi)
+                    if kind == "h":
+                        h_rows(g, lo, hi)
+        for g in range(2):
+            block("v", g, 0, 512)
+            v_rows(g, 0, 512)
 
-        def finish(nq, lo, hi):
-            res[nq, lo] = sb("y_sb%d_%d" % (nq, lo), [P, hi - lo], F32)
-            nc.scalar.activation(out=res[nq, lo][:], in_=accs["y", nq, lo][:, : hi - lo], func=ACT.Gelu_apprx_tanh, bias=b_sb[:, nq : nq + 1])
-            nc.sync.dma_start(out=out[nq * P : (nq + 1) * P, lo:hi], in_=res[nq, lo][:])
-
-
-        copy_in("w", 0, 0, "V", 0, 512)
-        quant_in("w", 0, 0)
-        copy_in("w", 0, 1, "S", 336, 512)
-        constants()
-        copy_in("w", 0, 1, "V", 0, 336)
-        quant_in("w", 0, 1)
-        copy_in("x", 0, 0, "S", 128, 256)
-        copy_in("x", 0, 0, "V", 0, 128)
+        for g in range(2):
+            for lo in (0, 512):
+                block("w", g, lo, lo + 512)
+        for lo in (0, 512):
+            shared_weave("w", 0, lo, lo + 336, lo + 512)
+        turn_vectors()
+        for lo in (0, 512):
+            quantize("w", 0, lo, lo + 512)
         scaled_offsets()
-        copy_in("x", 0, 1, "S", 176, 256)
-        spread_signs(0)
-        spread_signs(1)
-        quant_in("x", 0, 0)
-        stage1(0, 0, 256, 0, [0])
-        copy_in("x", 0, 1, "V", 0, 176)
-        quant_in("x", 0, 1)
-        stage1(0, 0, 256, 0, [1])
-        copy_in("x", 1, 0, "V", 0, 256)
-        evac(0, 0, 256, "SSSS")
-        quant_in("x", 1, 0)
-        stage1(0, 256, 512, 4, [0])
-        copy_in("x", 1, 1, "V", 0, 256)
-        quant_in("x", 1, 1)
-        stage1(0, 256, 512, 4, [1])
-        h_weave(0, 0)
-        evac(0, 256, 512, "SSSS")
-        h_quant(0, 0)
-        copy_in("w", 1, 0, "S", 384, 512)
-        copy_in("w", 1, 0, "V", 0, 384)
-        h_weave(0, 256)
-        quant_in("w", 1, 0)
-        stage1(1, 0, 512, 0, [0])
-        h_quant(0, 256)
-        copy_in("w", 1, 1, "S", 336, 512)
-        copy_in("w", 1, 1, "V", 0, 336)
-        quant_in("w", 1, 1)
-        stage1(1, 0, 512, 0, [1])
-
-        copy_in("x", 2, 0, "S", 0, 256)
-        evac(1, 0, 512, "SSSS")
-        copy_in("x", 2, 1, "V", 0, 256)
-        quant_in("x", 2, 0)
-        quant_in("x", 2, 1)
-        stage1(0, 512, 768, 4, [0, 1])
-        v_weave(0, 0, "V")
-        evac(0, 512, 768, "SSSS")
-        stage1(1, 512, 768, 0, [0, 1])
-        v_sign(0, 0)
-        v_weave(0, 1, "V")
-        v_quant(0, 0)
-        v_sign(0, 1)
-        evac(1, 512, 768, "SSSS")
-        h_weave(1, 0)
-        v_quant(0, 1)
-        h_quant(1, 0)
-        stage2(0, 0, 512, 4)
-        stage2(1, 0, 512, 5)
-        copy_in("x", 3, 0, "V", 0, 256)
-        copy_in("x", 3, 1, "V", 0, 256)
-        quant_in("x", 3, 0)
-        quant_in("x", 3, 1)
-        v_weave(1, 0, "S")
-        finish(0, 0, 512)
-        finish(1, 0, 512)
-        stage1(0, 768, 1024, 0, [0, 1])
-        stage1(1, 768, 1024, 4, [0, 1])
-        h_weave(0, 512)
-        h_weave(1, 512)
-        h_quant(0, 512)
-        h_quant(1, 512)
-        evac(0, 768, 1024, "SSSS")
-        stage2(0, 512, 768, 0)
-        stage2(1, 512, 768, 1)
-        v_weave(1, 1, "V")
-        v_sign(1, 0)
-        v_sign(1, 1)
-        v_quant(1, 0)
-        v_quant(1, 1)
-        evac(1, 768, 1024, "SSSS")
-        stage2(2, 0, 512, 2)
-        stage2(3, 0, 512, 3)
-        stage2(2, 512, 768, 4)
-        stage2(3, 512, 768, 5)
-        finish(0, 512, 768)
-        finish(1, 512, 768)
-        finish(2, 0, 512)
-        finish(3, 0, 512)
-        finish(2, 512, 768)
-        finish(3, 512, 768)
-        h_weave(0, 768)
-        h_weave(1, 768)
-        h_quant(0, 768)
-        h_quant(1, 768)
-        for nq in range(4):
-            stage2(nq, 768, 1024, [6, 7, 0, 1][nq])
-        for nq in range(4):
-            finish(nq, 768, 1024)
+        weave("S", "x", 0, *a)
+        shared_weave("w", 1, 0, 352, 512)
+        quantize("x", 0, *a)
+        product1(0, *a, [0, 1], [0])
+        product1(1, *a, [2, 3], [0])
+        weave("S", "w", 1, 720, 1024)
+        weave("V", "w", 1, 512, 592)
+        weave("V", "x", 1, *a)
+        quantize("w", 1, 0, 512)
+        quantize("x", 1, *a)
+        product1(0, *a, [0, 1], [1])
+        weave("V", "w", 1, 592, 720)
+        weave("S", "x", 0, *bb)
+        drain("S", 0, *a, range(4))
+        quantize("w", 1, 512, 1024)
+        product1(1, *a, [2, 3], [1])
+        weave("V", "x", 1, *bb)
+        quantize("x", 0, *bb)
+        quantize("x", 1, *bb)
+        product1(0, *bb, [4, 5])
+        product1(1, *bb, [6, 7])
+        drain("S", 1, *a, range(4))
+        weave("V", "x", 0, *c)
+        weave("V", "h", 0, *a)
+        quantize("x", 0, *c)
+        drain("S", 0, *bb, range(4))
+        product1(0, *c, [0, 1], [0])
+        product1(1, *c, [2, 3], [0])
+        weave("V", "x", 1, *c)
+        quantize("h", 0, *a)
+        quantize("x", 1, *c)
+        product1(0, *c, [0, 1], [1])
+        product1(1, *c, [2, 3], [1])
+        drain("S", 1, *bb, range(4))
+        weave("V", "h", 1, *a)
+        v_sign("V", 0, 0, 512, [0])
+        quantize("h", 1, *a)
+        v_sign("V", 0, 0, 512, [1, 2, 3])
+        drain("S", 0, *c, range(4))
+        weave("V", "h", 0, *bb)
+        weave("V", "v", 0, 0, 512)
+        drain("S", 1, *c, range(4))
+        quantize("h", 0, *bb)
+        v_sign("S", 1, 0, 512, [0, 1, 2])
+        quantize("v", 0, 0, 512)
+        product2(0, 512, [0, 1], [0], [0, 1])
+        weave("V", "x", 0, *d)
+        shared_weave("x", 1, 768, 896, 1024)
+        v_sign("S", 1, 0, 512, [3])
+        quantize("x", 0, *d)
+        quantize("x", 1, *d)
+        product1(0, *d, [4, 5])
+        product1(1, *d, [6, 7])
+        product2(0, 512, [2, 3], [0], [2, 3])
+        weave("V", "h", 1, *bb)
+        shared_weave("v", 1, 0, 352, 512)
+        drain("S", 0, *d, range(4))
+        quantize("h", 1, *bb)
+        quantize("v", 1, 0, 512)
+        product2(0, 512, [0, 1, 2, 3], [1])
+        weave("V", "h", 0, *c)
+        drain("S", 1, *d, range(4))
+        weave("V", "h", 1, *c)
+        quantize("h", 0, *c)
+        quantize("h", 1, *c)
+        product2(*c, [4, 5])
+        weave("V", "h", 0, *d)
+        finish(0, 512)
+        weave("V", "h", 1, *d)
+        finish(*c)
+        quantize("h", 0, *d)
+        product2(*d, [0, 1, 2, 3], [0])
+        quantize("h", 1, *d)
+        product2(*d, [0, 1, 2, 3], [1])
+        finish(*d)

@@ -32,11 +32,8 @@ def tile_mix_kern_arc_gelu_kernel(tc, x, w, cw, cb, v, b, out):
             return keep.tile(shape, dtype, name=name, align_bytes=64)
 
         hbm = {"w": w, "x": x, "v": v}
-        raw, woven, accs, rows = {}, {}, {}, {}
-        codes = {(kind, g): sb("%s_codes%d" % (kind, g), [P, width], U32)
-                 for kind, width in (("w", J), ("x", T), ("v", N), ("h", T)) for g in range(2)}
-        scales = {(kind, g): sb("%s_scales%d" % (kind, g), [P, width], U8)
-                  for kind, width in (("w", J), ("x", T), ("v", N), ("h", T)) for g in range(2)}
+        raw, woven, accs, rows, groups = {}, {}, {}, {}, {}
+        codes, pairs = {}, {}
 
         def load(kind, g, lo, hi):
             tile = sb("%s_raw%d_%d" % (kind, g, lo), [P, PACK, hi - lo], F32)
@@ -49,8 +46,29 @@ def tile_mix_kern_arc_gelu_kernel(tc, x, w, cw, cb, v, b, out):
                     return a, ap
             raise ValueError("no tile holds these columns")
 
-        def block(kind, g, lo, hi):
-            woven.setdefault((kind, g), []).append((lo, hi, sb("%s_woven%d_%d" % (kind, g, lo), [P, PACK * (hi - lo)], BF16)[:]))
+        def block(kind, lo, hi):
+            width = hi - lo
+            both = sb("%s_woven%d" % (kind, lo), [P, 2 * PACK * width], BF16)
+            words = sb("%s_codes%d" % (kind, lo), [P, 2 * width], U32)
+            planes = sb("%s_scales%d" % (kind, lo), [P, 2 * width], U8)
+            pairs[kind, lo] = (both, words, planes)
+            for g in range(2):
+                woven.setdefault((kind, g), []).append((lo, hi, both[:, g * PACK * width : (g + 1) * PACK * width]))
+                cols = slice(g * width, (g + 1) * width)
+                codes.setdefault((kind, g), []).append((lo, hi, (words[:, cols], planes[:, cols])))
+            if kind == "h":
+                pairs["rows", lo] = sb("h_rows%d" % lo, [P, PACK, 2 * width], BF16)
+                for g in range(2):
+                    rows.setdefault((kind, g), []).append((lo, hi, pairs["rows", lo][:, :, g * width : (g + 1) * width]))
+
+        def weave_h_both(lo):
+            dst = pairs["h", lo][0][:].rearrange("p (c i s) -> p c s i", i=RUN, s=PACK)
+            src = pairs["rows", lo][:].rearrange("p s (c i) -> p c s i", i=RUN)
+            nc.vector.tensor_scalar(out=dst, in0=src, scalar1=0.0, scalar2=None, op0=ALU.max)
+
+        def quantize_both(kind, lo):
+            both, words, planes = pairs[kind, lo]
+            nc.vector.quantize_mx(out=words[:].bitcast(FP8X4), scales=planes[:], in_=both[:])
 
         def weave(engine, kind, g, lo, hi):
             a, src = find(rows if (kind, g) in rows else raw, (kind, g), lo, hi)
@@ -73,16 +91,19 @@ def tile_mix_kern_arc_gelu_kernel(tc, x, w, cw, cb, v, b, out):
             weave("S", kind, g, cut, hi)
             weave("V", kind, g, lo, cut)
 
+        def operand(kind, g, lo, hi):
+            a, (words, planes) = find(codes, (kind, g), lo, hi)
+            return words[:, lo - a : hi - a].bitcast(FP8X4), planes[:, lo - a : hi - a]
+
         def quantize(kind, g, lo, hi):
             a, src = find(woven, (kind, g), lo, hi)
-            nc.vector.quantize_mx(out=codes[kind, g][:, lo:hi].bitcast(FP8X4), scales=scales[kind, g][:, lo:hi],
-                                  in_=src[:, PACK * (lo - a) : PACK * (hi - a)])
+            words, planes = operand(kind, g, lo, hi)
+            nc.vector.quantize_mx(out=words, scales=planes, in_=src[:, PACK * (lo - a) : PACK * (hi - a)])
 
         def mx_pass(acc, stationary, cols, moving, g, lo, hi, first, last):
-            nc.tensor.matmul_mx(
-                out=acc, lhsT=codes[stationary, g][:, cols].bitcast(FP8X4), lhsT_scale=scales[stationary, g][:, cols],
-                rhs=codes[moving, g][:, lo:hi].bitcast(FP8X4), rhs_scale=scales[moving, g][:, lo:hi], start=first, stop=last,
-            )
+            lhs, lhs_scale = operand(stationary, g, cols.start, cols.stop)
+            rhs, rhs_scale = operand(moving, g, lo, hi)
+            nc.tensor.matmul_mx(out=acc, lhsT=lhs, lhsT_scale=lhs_scale, rhs=rhs, rhs_scale=rhs_scale, start=first, stop=last)
 
         def product1(jg, lo, hi, banks, passes=(0, 1)):
             per = PACK // len(banks)
@@ -96,9 +117,6 @@ def tile_mix_kern_arc_gelu_kernel(tc, x, w, cw, cb, v, b, out):
                         u = n * per + m
                         cols = slice(jg * PASS + u * P, jg * PASS + (u + 1) * P)
                         mx_pass(accs["d", jg, lo, u], "w", cols, "x", g, lo, hi, g == 0 and m == 0, g == 1 and m == per - 1)
-
-        def h_rows(jg, lo, hi):
-            rows.setdefault(("h", jg), []).append((lo, hi, sb("h_rows%d_%d" % (jg, lo), [P, PACK, hi - lo], BF16)[:]))
 
         def drain(engine, jg, lo, hi, slots):
             a, dst = find(rows, ("h", jg), lo, hi)
@@ -124,23 +142,31 @@ def tile_mix_kern_arc_gelu_kernel(tc, x, w, cw, cb, v, b, out):
                     nc.vector.tensor_scalar(out=dst[:, s, lo - c : hi - c], in0=src[:, s, lo - a : hi - a], scalar1=sign[:, g, s : s + 1],
                                             scalar2=None, op0=ALU.mult)
 
-        def product2(lo, hi, banks, passes=(0, 1), tiles=range(PACK)):
-            per = len(tiles) // len(banks)
+        def y_banks(lo, hi, banks):
+            per = PACK // len(banks)
             for n, bank in enumerate(banks):
-                if passes[0] == 0:
-                    tile = psum.tile([P, per, BANK // per], F32, name="y%d_%d" % (lo, tiles[n * per]), tag="bank%d" % bank)
-                    for m in range(per):
-                        accs["y", tiles[n * per + m], lo] = tile[:, m, : hi - lo]
-                for g in passes:
-                    for m in range(per):
-                        q = tiles[n * per + m]
-                        mx_pass(accs["y", q, lo], "v", slice(q * P, (q + 1) * P), "h", g, lo, hi, g == 0 and m == 0, g == 1 and m == per - 1)
+                tile = psum.tile([P, per, BANK // per], F32, name="y%d_%d" % (lo, n), tag="bank%d" % bank)
+                group = {"left": 2 * per * (hi - lo), "open": False}
+                for m in range(per):
+                    accs["y", n * per + m, lo] = tile[:, m, : hi - lo]
+                    groups[n * per + m, lo] = group
 
-        def finish(lo, hi, tiles=range(PACK)):
+        def product2(base, lo, hi, passes=(0, 1), tiles=range(PACK)):
             for q in tiles:
-                res = sb("y_sb%d_%d" % (q, lo), [P, hi - lo], F32)
-                nc.scalar.activation(out=res[:], in_=accs["y", q, lo], func=ACT.Gelu_apprx_tanh, bias=b_sb[:, q : q + 1])
-                nc.sync.dma_start(out=out[q * P : (q + 1) * P, lo:hi], in_=res[:])
+                for g in passes:
+                    group = groups[q, base]
+                    group["left"] = group["left"] - (hi - lo)
+                    mx_pass(accs["y", q, base][:, lo - base : hi - base], "v", slice(q * P, (q + 1) * P), "h", g, lo, hi,
+                            not group["open"], group["left"] == 0)
+                    group["open"] = True
+
+        def finish(lo, hi, group=1, tiles=range(PACK)):
+            for n, q in enumerate(tiles):
+                if n % group == 0:
+                    res = sb("y_sb%d_%d" % (q, lo), [P, group, hi - lo], F32)
+                nc.scalar.activation(out=res[:, n % group, :], in_=accs["y", q, lo], func=ACT.Gelu_apprx_tanh, bias=b_sb[:, q : q + 1])
+                if n % group == group - 1:
+                    nc.sync.dma_start(out=out.rearrange("(q p) t -> p q t", p=P)[:, q + 1 - group : q + 1, lo:hi], in_=res[:])
 
         cb_sb = sb("cb_sb", [P, 2, PACK], F32)
         b_sb = sb("b_sb", [P, PACK], F32)
@@ -185,29 +211,23 @@ def tile_mix_kern_arc_gelu_kernel(tc, x, w, cw, cb, v, b, out):
         load("x", 0, *a)
         load("w", 1, 0, 1024)
         load("x", 1, *a)
-        for lo, hi in (bb, c):
-            for g in range(2):
-                load("x", g, lo, hi)
         for g in range(2):
+            load("x", g, *bb)
+        for g, (lo, hi) in enumerate((c, d)):
             load("v", g, 0, 512)
-        for g in range(2):
-            load("x", g, *d)
+            load("x", 0, lo, hi)
+            load("x", 1, lo, hi)
         warm_table()
-        for kind in "xh":
-            for g in range(2):
-                for lo, hi in (a, bb, c, d):
-                    block(kind, g, lo, hi)
-                    if kind == "h":
-                        h_rows(g, lo, hi)
-        for g in range(2):
-            block("v", g, 0, 512)
-            v_rows(g, 0, 512)
-
-        for g in range(2):
-            for lo in (0, 512):
-                block("w", g, lo, lo + 512)
+        for lo, hi in (a, bb, c, d):
+            block("x", lo, hi)
+            block("h", lo, hi)
         for lo in (0, 512):
-            shared_weave("w", 0, lo, lo + 336, lo + 512)
+            block("w", lo, lo + 512)
+        block("v", 0, 512)
+        for g in range(2):
+            v_rows(g, 0, 512)
+        for lo in (0, 512):
+            shared_weave("w", 0, lo, lo + 352, lo + 512)
         turn_vectors()
         for lo in (0, 512):
             quantize("w", 0, lo, lo + 512)
@@ -234,56 +254,58 @@ def tile_mix_kern_arc_gelu_kernel(tc, x, w, cw, cb, v, b, out):
         product1(0, *bb, [4, 5])
         product1(1, *bb, [6, 7])
         drain("S", 1, *a, range(4))
-        weave("V", "x", 0, *c)
         weave("V", "h", 0, *a)
-        quantize("x", 0, *c)
+        v_sign("V", 0, 0, 512)
         drain("S", 0, *bb, range(4))
-        product1(0, *c, [0, 1], [0])
-        product1(1, *c, [2, 3], [0])
-        weave("V", "x", 1, *c)
-        quantize("h", 0, *a)
-        quantize("x", 1, *c)
-        product1(0, *c, [0, 1], [1])
-        product1(1, *c, [2, 3], [1])
-        drain("S", 1, *bb, range(4))
         weave("V", "h", 1, *a)
-        v_sign("V", 0, 0, 512, [0])
-        quantize("h", 1, *a)
-        v_sign("V", 0, 0, 512, [1, 2, 3])
-        drain("S", 0, *c, range(4))
-        weave("V", "h", 0, *bb)
-        weave("V", "v", 0, 0, 512)
-        drain("S", 1, *c, range(4))
-        quantize("h", 0, *bb)
-        v_sign("S", 1, 0, 512, [0, 1, 2])
+        weave("V", "x", 0, *c)
+        drain("S", 1, *bb, range(4))
+        quantize_both("h", 0)
+        weave("V", "x", 1, *c)
+        weave("S", "h", 0, *bb)
+        quantize("x", 0, *c)
+        quantize("x", 1, *c)
+        product1(0, *c, [0, 1])
+        product1(1, *c, [2, 3])
+        shared_weave("v", 0, 0, 320, 512)
+        v_sign("S", 1, 0, 512, [2, 3])
+        v_sign("V", 1, 0, 512, [0, 1])
         quantize("v", 0, 0, 512)
-        product2(0, 512, [0, 1], [0], [0, 1])
+        y_banks(0, 512, [4, 5, 6, 7])
+        product2(0, *a, [0])
         weave("V", "x", 0, *d)
-        shared_weave("x", 1, 768, 896, 1024)
-        v_sign("S", 1, 0, 512, [3])
-        quantize("x", 0, *d)
-        quantize("x", 1, *d)
-        product1(0, *d, [4, 5])
-        product1(1, *d, [6, 7])
-        product2(0, 512, [2, 3], [0], [2, 3])
+        drain("S", 0, *c, range(4))
         weave("V", "h", 1, *bb)
-        shared_weave("v", 1, 0, 352, 512)
-        drain("S", 0, *d, range(4))
-        quantize("h", 1, *bb)
-        quantize("v", 1, 0, 512)
-        product2(0, 512, [0, 1, 2, 3], [1])
+        quantize("x", 0, *d)
+        product1(0, *d, [0, 1], [0])
+        drain("S", 1, *c, range(4))
+        weave("V", "x", 1, *d)
+        quantize_both("h", 256)
+        product1(1, *d, [2, 3], [0])
+        quantize("x", 1, *d)
+        product1(0, *d, [0, 1], [1])
+        product1(1, *d, [2, 3], [1])
+        product2(0, *bb, [0])
+        shared_weave("v", 1, 0, 256, 512)
         weave("V", "h", 0, *c)
-        drain("S", 1, *d, range(4))
+        quantize("v", 1, 0, 512)
+        for q in range(4):
+            product2(0, *a, [1], [q])
+            product2(0, *bb, [1], [q])
+        drain("S", 0, *d, range(4))
+        drain("S", 1, *d, [0, 1])
         weave("V", "h", 1, *c)
-        quantize("h", 0, *c)
-        quantize("h", 1, *c)
-        product2(*c, [4, 5])
+        drain("V", 1, *d, [2, 3])
+        quantize_both("h", 512)
+        finish(0, 512, 1)
+        y_banks(512, 768, [0, 1])
+        product2(512, *c)
         weave("V", "h", 0, *d)
-        finish(0, 512)
         weave("V", "h", 1, *d)
-        finish(*c)
+        finish(*c, 2)
         quantize("h", 0, *d)
-        product2(*d, [0, 1, 2, 3], [0])
+        y_banks(768, 1024, [2, 3, 4, 5])
+        product2(768, *d, [0])
         quantize("h", 1, *d)
-        product2(*d, [0, 1, 2, 3], [1])
-        finish(*d)
+        product2(768, *d, [1])
+        finish(*d, 1)

@@ -203,7 +203,6 @@ def tile_mix_kern_arc_gelu_kernel(tc, x, w, cw, cb, v, b, out):
             warm2 = sb("warm2", [P, 1], F32)
             nc.scalar.activation(out=warm2[:], in_=ident[:, 0:1], func=ACT.Gelu_apprx_tanh)
 
-
         prepare()
         load("w", 0, 0, 1024)
         load_vectors()
@@ -286,16 +285,17 @@ def tile_mix_kern_arc_gelu_kernel(tc, x, w, cw, cb, v, b, out):
         product1(0, *d, [0, 1], [1])
         product1(1, *d, [2, 3], [1])
         product2(0, *bb, [0])
-        shared_weave("v", 1, 0, 256, 512)
+        shared_weave("v", 1, 0, 320, 512)
         weave("V", "h", 0, *c)
-        quantize("v", 1, 0, 512)
-        for q in range(4):
-            product2(0, *a, [1], [q])
-            product2(0, *bb, [1], [q])
+        for half in range(2):
+            quantize("v", 1, 256 * half, 256 * half + 256)
+            for q in (2 * half, 2 * half + 1):
+                product2(0, *a, [1], [q])
+                product2(0, *bb, [1], [q])
         drain("S", 0, *d, range(4))
-        drain("S", 1, *d, [0, 1])
+        drain("S", 1, *d, [0])
         weave("V", "h", 1, *c)
-        drain("V", 1, *d, [2, 3])
+        drain("V", 1, *d, [2, 3, 1])
         quantize_both("h", 512)
         finish(0, 512, 1)
         y_banks(512, 768, [0, 1])
@@ -305,7 +305,8 @@ def tile_mix_kern_arc_gelu_kernel(tc, x, w, cw, cb, v, b, out):
         finish(*c, 2)
         quantize("h", 0, *d)
         y_banks(768, 1024, [2, 3, 4, 5])
-        product2(768, *d, [0])
+        product2(768, *d, [0], [0, 1])
         quantize("h", 1, *d)
-        product2(768, *d, [1])
+        product2(768, *d, [1], [0, 1])
+        product2(768, *d, [0, 1], [2, 3])
         finish(*d, 1)

@@ -32,8 +32,7 @@ def tile_mix_kern_arc_gelu_kernel(tc, x, w, cw, cb, v, b, out):
             return keep.tile(shape, dtype, name=name, align_bytes=64)
 
         hbm = {"w": w, "x": x, "v": v}
-        raw, woven, accs, rows, groups = {}, {}, {}, {}, {}
-        codes, pairs = {}, {}
+        raw, woven, accs, rows, groups, codes, pairs = {}, {}, {}, {}, {}, {}, {}
 
         def load(kind, g, lo, hi):
             tile = sb("%s_raw%d_%d" % (kind, g, lo), [P, PACK, hi - lo], F32)
@@ -56,10 +55,16 @@ def tile_mix_kern_arc_gelu_kernel(tc, x, w, cw, cb, v, b, out):
                 woven.setdefault((kind, g), []).append((lo, hi, both[:, g * PACK * width : (g + 1) * PACK * width]))
                 cols = slice(g * width, (g + 1) * width)
                 codes.setdefault((kind, g), []).append((lo, hi, (words[:, cols], planes[:, cols])))
-            if kind == "h":
-                pairs["rows", lo] = sb("h_rows%d" % lo, [P, PACK, 2 * width], BF16)
-                for g in range(2):
-                    rows.setdefault((kind, g), []).append((lo, hi, pairs["rows", lo][:, :, g * width : (g + 1) * width]))
+
+        def row_tiles(kind, lo, hi):
+            for g in range(2):
+                rows.setdefault((kind, g), []).append((lo, hi, sb("%s_rows%d_%d" % (kind, g, lo), [P, PACK, hi - lo], BF16)[:]))
+
+        def joint_rows(lo, hi):
+            width = hi - lo
+            pairs["rows", lo] = sb("h_rows_%d" % lo, [P, PACK, 2 * width], BF16)
+            for g in range(2):
+                rows.setdefault(("h", g), []).append((lo, hi, pairs["rows", lo][:, :, g * width : (g + 1) * width]))
 
         def weave_h_both(lo):
             dst = pairs["h", lo][0][:].rearrange("p (c i s) -> p c s i", i=RUN, s=PACK)
@@ -105,9 +110,11 @@ def tile_mix_kern_arc_gelu_kernel(tc, x, w, cw, cb, v, b, out):
             rhs, rhs_scale = operand(moving, g, lo, hi)
             nc.tensor.matmul_mx(out=acc, lhsT=lhs, lhsT_scale=lhs_scale, rhs=rhs, rhs_scale=rhs_scale, start=first, stop=last)
 
-        def product1(jg, lo, hi, banks, passes=(0, 1)):
+        def product1(jg, lo, hi, banks, passes=(0, 1), only=None):
             per = PACK // len(banks)
             for n, bank in enumerate(banks):
+                if only is not None and n not in only:
+                    continue
                 if passes[0] == 0:
                     tile = psum.tile([P, per, BANK // per], F32, name="d%d_%d_%d" % (jg, lo, n), tag="bank%d" % bank)
                     for m in range(per):
@@ -118,7 +125,7 @@ def tile_mix_kern_arc_gelu_kernel(tc, x, w, cw, cb, v, b, out):
                         cols = slice(jg * PASS + u * P, jg * PASS + (u + 1) * P)
                         mx_pass(accs["d", jg, lo, u], "w", cols, "x", g, lo, hi, g == 0 and m == 0, g == 1 and m == per - 1)
 
-        def drain(engine, jg, lo, hi, slots):
+        def drain(engine, jg, lo, hi, slots=range(PACK)):
             a, dst = find(rows, ("h", jg), lo, hi)
             for u in slots:
                 src = accs["d", jg, lo, u]
@@ -129,18 +136,14 @@ def tile_mix_kern_arc_gelu_kernel(tc, x, w, cw, cb, v, b, out):
                     nc.scalar.activation(out=dst[:, u, lo - a : hi - a], in_=src, func=ACT.Relu,
                                          bias=shift[:, jg, u : u + 1], scale=gain[:, jg, u : u + 1])
 
-        def v_rows(g, lo, hi):
-            rows.setdefault(("v", g), []).append((lo, hi, sb("v_rows%d_%d" % (g, lo), [P, PACK, hi - lo], BF16)[:]))
-
-        def v_sign(engine, g, lo, hi, slots=range(PACK)):
-            a, src = find(raw, ("v", g), lo, hi)
-            c, dst = find(rows, ("v", g), lo, hi)
+        def v_sign(engine, g, slots=range(PACK)):
+            a, src = find(raw, ("v", g), 0, N)
+            c, dst = find(rows, ("v", g), 0, N)
             for s in slots:
                 if engine == "S":
-                    nc.scalar.activation(out=dst[:, s, lo - c : hi - c], in_=src[:, s, lo - a : hi - a], func=ACT.Copy, scale=sign[:, g, s : s + 1])
+                    nc.scalar.activation(out=dst[:, s, :], in_=src[:, s, :], func=ACT.Copy, scale=sign[:, g, s : s + 1])
                 else:
-                    nc.vector.tensor_scalar(out=dst[:, s, lo - c : hi - c], in0=src[:, s, lo - a : hi - a], scalar1=sign[:, g, s : s + 1],
-                                            scalar2=None, op0=ALU.mult)
+                    nc.vector.tensor_scalar(out=dst[:, s, :], in0=src[:, s, :], scalar1=sign[:, g, s : s + 1], scalar2=None, op0=ALU.mult)
 
         def y_banks(lo, hi, banks):
             per = PACK // len(banks)
@@ -195,116 +198,119 @@ def tile_mix_kern_arc_gelu_kernel(tc, x, w, cw, cb, v, b, out):
         def scaled_offsets():
             nc.vector.tensor_tensor(out=shift[:], in0=cb_sb[:], in1=gain[:], op=ALU.mult)
 
-        def prepare():
-            nc.vector.memset(stage[:], 0.0)
-            make_identity(nc, ident[:])
-
         def warm_table():
-            warm2 = sb("warm2", [P, 1], F32)
-            nc.scalar.activation(out=warm2[:], in_=ident[:, 0:1], func=ACT.Gelu_apprx_tanh)
+            warm = sb("warm", [P, 1], F32)
+            nc.scalar.activation(out=warm[:], in_=ident[:, 0:1], func=ACT.Gelu_apprx_tanh)
 
-        prepare()
+        nc.vector.memset(stage[:], 0.0)
+        make_identity(nc, ident[:])
+
+        a, bb, c, d = (0, 256), (256, 512), (512, 768), (768, 1024)
+        d0, d1 = (768, 896), (896, 1024)
         load("w", 0, 0, 1024)
         load_vectors()
-        a, bb, c, d = [(lo, lo + 256) for lo in range(0, T, 256)]
-        load("x", 0, *a)
+        load("v", 0, 0, 512)
         load("w", 1, 0, 1024)
-        load("x", 1, *a)
-        for g in range(2):
-            load("x", g, *bb)
-        for g, (lo, hi) in enumerate((c, d)):
-            load("v", g, 0, 512)
+        for lo, hi in (a, bb, c, d):
             load("x", 0, lo, hi)
             load("x", 1, lo, hi)
+        load("v", 1, 0, 512)
         warm_table()
         for lo, hi in (a, bb, c, d):
             block("x", lo, hi)
             block("h", lo, hi)
+            row_tiles("h", lo, hi)
         for lo in (0, 512):
             block("w", lo, lo + 512)
         block("v", 0, 512)
-        for g in range(2):
-            v_rows(g, 0, 512)
+        row_tiles("v", 0, 512)
         for lo in (0, 512):
             shared_weave("w", 0, lo, lo + 352, lo + 512)
         turn_vectors()
         for lo in (0, 512):
             quantize("w", 0, lo, lo + 512)
         scaled_offsets()
-        weave("S", "x", 0, *a)
+        v_sign("S", 0, [3])
+        v_sign("V", 0, [0, 1, 2])
+        shared_weave("v", 0, 0, 352, 512)
+        quantize("v", 0, 0, 512)
         shared_weave("w", 1, 0, 352, 512)
+        shared_weave("w", 1, 512, 736, 1024)
+        weave("V", "x", 0, *a)
+        quantize("w", 1, 0, 512)
         quantize("x", 0, *a)
         product1(0, *a, [0, 1], [0])
-        product1(1, *a, [2, 3], [0])
-        weave("S", "w", 1, 720, 1024)
-        weave("V", "w", 1, 512, 592)
-        weave("V", "x", 1, *a)
-        quantize("w", 1, 0, 512)
+        shared_weave("x", 1, 0, 128, 256)
+        quantize("w", 1, 512, 1024)
         quantize("x", 1, *a)
         product1(0, *a, [0, 1], [1])
-        weave("V", "w", 1, 592, 720)
-        weave("S", "x", 0, *bb)
-        drain("S", 0, *a, range(4))
-        quantize("w", 1, 512, 1024)
-        product1(1, *a, [2, 3], [1])
-        weave("V", "x", 1, *bb)
+        product1(1, *a, [2, 3])
+        shared_weave("x", 0, 256, 448, 512)
+        drain("S", 0, *a)
         quantize("x", 0, *bb)
+        product1(0, *bb, [4, 5], [0])
+        weave("V", "x", 1, *bb)
+        drain("S", 1, *a)
         quantize("x", 1, *bb)
-        product1(0, *bb, [4, 5])
+        product1(0, *bb, [4, 5], [1])
         product1(1, *bb, [6, 7])
-        drain("S", 1, *a, range(4))
         weave("V", "h", 0, *a)
-        v_sign("V", 0, 0, 512)
-        drain("S", 0, *bb, range(4))
-        weave("V", "h", 1, *a)
         weave("V", "x", 0, *c)
-        drain("S", 1, *bb, range(4))
-        quantize_both("h", 0)
-        weave("V", "x", 1, *c)
-        weave("S", "h", 0, *bb)
+        drain("S", 0, *bb)
+        quantize("h", 0, *a)
         quantize("x", 0, *c)
+        product1(0, *c, [0, 1], [0])
+        weave("V", "x", 1, *c)
+        weave("V", "h", 1, *a)
         quantize("x", 1, *c)
-        product1(0, *c, [0, 1])
+        product1(0, *c, [0, 1], [1])
         product1(1, *c, [2, 3])
-        shared_weave("v", 0, 0, 320, 512)
-        v_sign("S", 1, 0, 512, [2, 3])
-        v_sign("V", 1, 0, 512, [0, 1])
-        quantize("v", 0, 0, 512)
-        y_banks(0, 512, [4, 5, 6, 7])
-        product2(0, *a, [0])
+        drain("S", 1, *bb)
+        weave("S", "h", 0, 384, 512)
+
         weave("V", "x", 0, *d)
-        drain("S", 0, *c, range(4))
-        weave("V", "h", 1, *bb)
+        drain("S", 0, *c)
+        quantize("h", 1, *a)
         quantize("x", 0, *d)
         product1(0, *d, [0, 1], [0])
-        drain("S", 1, *c, range(4))
+        y_banks(0, 512, [4, 5, 6, 7])
+        product2(0, *a, [0])
         weave("V", "x", 1, *d)
-        quantize_both("h", 256)
-        product1(1, *d, [2, 3], [0])
+        weave("V", "h", 0, 256, 384)
         quantize("x", 1, *d)
+        drain("S", 1, *c)
         product1(0, *d, [0, 1], [1])
-        product1(1, *d, [2, 3], [1])
+        product1(1, *d, [2, 3])
+        weave("V", "h", 1, *bb)
+        quantize("h", 0, *bb)
         product2(0, *bb, [0])
-        shared_weave("v", 1, 0, 320, 512)
-        weave("V", "h", 0, *c)
+
+        v_sign("S", 1, [3])
+        v_sign("V", 1, [0, 1, 2])
+        drain("S", 0, *d)
+        quantize("h", 1, *bb)
+        weave("V", "v", 1, 0, 256)
+        drain("S", 1, *d)
+        weave("V", "v", 1, 256, 512)
         for half in range(2):
             quantize("v", 1, 256 * half, 256 * half + 256)
             for q in (2 * half, 2 * half + 1):
                 product2(0, *a, [1], [q])
                 product2(0, *bb, [1], [q])
-        drain("S", 0, *d, range(4))
-        drain("S", 1, *d, [0])
-        weave("V", "h", 1, *c)
-        drain("V", 1, *d, [2, 3, 1])
-        quantize_both("h", 512)
         finish(0, 512, 1)
-        y_banks(512, 768, [0, 1])
-        product2(512, *c)
+        weave("V", "h", 0, *c)
+        weave("V", "h", 1, *c)
+        quantize("h", 0, *c)
+        quantize("h", 1, *c)
+        y_banks(*c, [0, 1])
+        product2(512, *c, [0])
+        product2(512, *c, [1])
+
         weave("V", "h", 0, *d)
         weave("V", "h", 1, *d)
         finish(*c, 2)
         quantize("h", 0, *d)
-        y_banks(768, 1024, [2, 3, 4, 5])
+        y_banks(*d, [2, 3, 4, 5])
         product2(768, *d, [0], [0, 1])
         quantize("h", 1, *d)
         product2(768, *d, [1], [0, 1])

@@ -206,7 +206,6 @@ def tile_mix_kern_arc_gelu_kernel(tc, x, w, cw, cb, v, b, out):
         make_identity(nc, ident[:])
 
         a, bb, c, d = (0, 256), (256, 512), (512, 768), (768, 1024)
-        d0, d1 = (768, 896), (896, 1024)
         load("w", 0, 0, 1024)
         load_vectors()
         load("v", 0, 0, 512)
@@ -215,6 +214,7 @@ def tile_mix_kern_arc_gelu_kernel(tc, x, w, cw, cb, v, b, out):
             load("x", 0, lo, hi)
             load("x", 1, lo, hi)
         load("v", 1, 0, 512)
+
         warm_table()
         for lo, hi in (a, bb, c, d):
             block("x", lo, hi)
@@ -230,87 +230,90 @@ def tile_mix_kern_arc_gelu_kernel(tc, x, w, cw, cb, v, b, out):
         for lo in (0, 512):
             quantize("w", 0, lo, lo + 512)
         scaled_offsets()
+
         v_sign("S", 0, [3])
         v_sign("V", 0, [0, 1, 2])
         shared_weave("v", 0, 0, 352, 512)
         quantize("v", 0, 0, 512)
+
         shared_weave("w", 1, 0, 352, 512)
         shared_weave("w", 1, 512, 736, 1024)
         weave("V", "x", 0, *a)
         quantize("w", 1, 0, 512)
         quantize("x", 0, *a)
-        product1(0, *a, [0, 1], [0])
-        shared_weave("x", 1, 0, 128, 256)
-        quantize("w", 1, 512, 1024)
+        product1(0, *a, [0, 1, 2, 3], [0])
+        shared_weave("x", 1, 0, 176, 256)
+        quantize("w", 1, 512, 768)
         quantize("x", 1, *a)
-        product1(0, *a, [0, 1], [1])
-        product1(1, *a, [2, 3])
-        shared_weave("x", 0, 256, 448, 512)
+        product1(0, *a, [0, 1, 2, 3], [1])
+        quantize("w", 1, 768, 1024)
+        product1(1, *a, [4, 5])
+        weave("V", "x", 0, *bb)
         drain("S", 0, *a)
         quantize("x", 0, *bb)
-        product1(0, *bb, [4, 5], [0])
+        product1(0, *bb, [6, 7], [0])
         weave("V", "x", 1, *bb)
         drain("S", 1, *a)
         quantize("x", 1, *bb)
-        product1(0, *bb, [4, 5], [1])
-        product1(1, *bb, [6, 7])
+        product1(0, *bb, [6, 7], [1])
+        product1(1, *bb, [0, 1])
         weave("V", "h", 0, *a)
         weave("V", "x", 0, *c)
         drain("S", 0, *bb)
         quantize("h", 0, *a)
         quantize("x", 0, *c)
-        product1(0, *c, [0, 1], [0])
+        product1(0, *c, [2, 3], [0])
         weave("V", "x", 1, *c)
         weave("V", "h", 1, *a)
         quantize("x", 1, *c)
-        product1(0, *c, [0, 1], [1])
-        product1(1, *c, [2, 3])
+        product1(0, *c, [2, 3], [1])
+        product1(1, *c, [4, 5])
         drain("S", 1, *bb)
         weave("S", "h", 0, 384, 512)
-
         weave("V", "x", 0, *d)
         drain("S", 0, *c)
         quantize("h", 1, *a)
         quantize("x", 0, *d)
-        product1(0, *d, [0, 1], [0])
-        y_banks(0, 512, [4, 5, 6, 7])
-        product2(0, *a, [0])
+        product1(0, *d, [6, 7], [0])
         weave("V", "x", 1, *d)
         weave("V", "h", 0, 256, 384)
         quantize("x", 1, *d)
         drain("S", 1, *c)
-        product1(0, *d, [0, 1], [1])
-        product1(1, *d, [2, 3])
+        product1(0, *d, [6, 7], [1])
+        product1(1, *d, [0, 1])
         weave("V", "h", 1, *bb)
         quantize("h", 0, *bb)
+        y_banks(0, 512, [2, 3, 4, 5])
+        product2(0, *a, [0])
         product2(0, *bb, [0])
 
-        v_sign("S", 1, [3])
-        v_sign("V", 1, [0, 1, 2])
+        v_sign("V", 1)
         drain("S", 0, *d)
         quantize("h", 1, *bb)
-        weave("V", "v", 1, 0, 256)
         drain("S", 1, *d)
-        weave("V", "v", 1, 256, 512)
-        for half in range(2):
-            quantize("v", 1, 256 * half, 256 * half + 256)
-            for q in (2 * half, 2 * half + 1):
-                product2(0, *a, [1], [q])
-                product2(0, *bb, [1], [q])
+        weave("S", "h", 0, 704, 768)
+        weave("V", "v", 1, 0, 128)
+        for q in range(4):
+            if q < 3:
+                weave("V", "v", 1, 128 * q + 128, 128 * q + 256)
+            else:
+                weave("V", "h", 0, 512, 704)
+            quantize("v", 1, 128 * q, 128 * q + 128)
+            product2(0, *a, [1], [q])
+            product2(0, *bb, [1], [q])
         finish(0, 512, 1)
-        weave("V", "h", 0, *c)
         weave("V", "h", 1, *c)
         quantize("h", 0, *c)
         quantize("h", 1, *c)
-        y_banks(*c, [0, 1])
-        product2(512, *c, [0])
-        product2(512, *c, [1])
-
+        y_banks(*c, [6, 7])
+        for pair in ([0, 1], [2, 3]):
+            product2(512, *c, [0], pair)
+            product2(512, *c, [1], pair)
         weave("V", "h", 0, *d)
         weave("V", "h", 1, *d)
-        finish(*c, 2)
+        finish(*c, 1)
         quantize("h", 0, *d)
-        y_banks(*d, [2, 3, 4, 5])
+        y_banks(*d, [0, 1, 2, 3])
         product2(768, *d, [0], [0, 1])
         quantize("h", 1, *d)
         product2(768, *d, [1], [0, 1])

@@ -145,6 +145,14 @@ def tile_mix_kern_arc_gelu_kernel(tc, x, w, cw, cb, v, b, out):
                 else:
                     nc.vector.tensor_scalar(out=dst[:, s, :], in0=src[:, s, :], scalar1=sign[:, g, s : s + 1], scalar2=None, op0=ALU.mult)
 
+        def weave_signed(g, lo, hi):
+            a, src = find(raw, ("v", g), lo, hi)
+            c, dst = find(woven, ("v", g), lo, hi)
+            dst = dst[:, PACK * (lo - c) : PACK * (hi - c)].rearrange("p (c i s) -> p c s i", i=RUN, s=PACK)
+            src = src[:, :, lo - a : hi - a].rearrange("p s (c i) -> p c s i", i=RUN)
+            signs = sign_run[:, g, :, :].unsqueeze(1).to_broadcast([P, (hi - lo) // RUN, PACK, RUN])
+            nc.vector.tensor_tensor(out=dst, in0=src, in1=signs, op=ALU.mult)
+
         def y_banks(lo, hi, banks):
             per = PACK // len(banks)
             for n, bank in enumerate(banks):
@@ -174,6 +182,7 @@ def tile_mix_kern_arc_gelu_kernel(tc, x, w, cw, cb, v, b, out):
         cb_sb = sb("cb_sb", [P, 2, PACK], F32)
         b_sb = sb("b_sb", [P, PACK], F32)
         sign = sb("sign", [P, 2, PACK], F32)
+        sign_run = sb("sign_run", [P, 2, PACK, RUN], F32)
         gain = sb("gain", [P, 2, PACK], F32)
         shift = sb("shift", [P, 2, PACK], F32)
         stage = sb("stage", [P, PASS], F32)
@@ -197,10 +206,25 @@ def tile_mix_kern_arc_gelu_kernel(tc, x, w, cw, cb, v, b, out):
 
         def scaled_offsets():
             nc.vector.tensor_tensor(out=shift[:], in0=cb_sb[:], in1=gain[:], op=ALU.mult)
+            nc.vector.tensor_copy(out=sign_run[:], in_=sign[:].unsqueeze(3).to_broadcast([P, 2, PACK, RUN]))
 
         def warm_table():
             warm = sb("warm", [P, 1], F32)
             nc.scalar.activation(out=warm[:], in_=ident[:, 0:1], func=ACT.Gelu_apprx_tanh)
+
+        def warm_operand():
+            ones = sb("warm_values", [P, PACK * 256], BF16)
+            nc.gpsimd.memset(ones[:], 1.0)
+            block_tiles = (ones, sb("warm_codes", [P, 256], U32), sb("warm_scales", [P, 256], U8))
+            pairs["warm", 0] = block_tiles
+
+        def warm_array(count, bank):
+            quantize_both("warm", 0)
+            ones, words, planes = pairs["warm", 0]
+            sink = psum.tile([P, 256], F32, name="warm_sink", tag="bank%d" % bank)
+            for n in range(count):
+                nc.tensor.matmul_mx(out=sink[:], lhsT=words[:, 0:P].bitcast(FP8X4), lhsT_scale=planes[:, 0:P],
+                                    rhs=words[:].bitcast(FP8X4), rhs_scale=planes[:], start=True, stop=True)
 
         nc.vector.memset(stage[:], 0.0)
         make_identity(nc, ident[:])
@@ -216,6 +240,7 @@ def tile_mix_kern_arc_gelu_kernel(tc, x, w, cw, cb, v, b, out):
         load("v", 1, 0, 512)
 
         warm_table()
+        warm_operand()
         for lo, hi in (a, bb, c, d):
             block("x", lo, hi)
             block("h", lo, hi)
@@ -235,6 +260,7 @@ def tile_mix_kern_arc_gelu_kernel(tc, x, w, cw, cb, v, b, out):
         v_sign("V", 0, [0, 1, 2])
         shared_weave("v", 0, 0, 352, 512)
         quantize("v", 0, 0, 512)
+        warm_array(8, 7)
 
         shared_weave("w", 1, 0, 352, 512)
         shared_weave("w", 1, 512, 736, 1024)
@@ -242,67 +268,63 @@ def tile_mix_kern_arc_gelu_kernel(tc, x, w, cw, cb, v, b, out):
         quantize("w", 1, 0, 512)
         quantize("x", 0, *a)
         product1(0, *a, [0, 1, 2, 3], [0])
+        product1(1, *a, [4, 5], [0])
         shared_weave("x", 1, 0, 176, 256)
         quantize("w", 1, 512, 768)
         quantize("x", 1, *a)
         product1(0, *a, [0, 1, 2, 3], [1])
         quantize("w", 1, 768, 1024)
-        product1(1, *a, [4, 5])
-        weave("V", "x", 0, *bb)
-        drain("S", 0, *a)
-        quantize("x", 0, *bb)
-        product1(0, *bb, [6, 7], [0])
+        product1(1, *a, [4, 5], [1])
+        shared_weave("x", 0, 256, 368, 512)
+        drain("V", 0, *a, [0, 1])
+        drain("S", 0, *a, [2, 3])
         weave("V", "x", 1, *bb)
         drain("S", 1, *a)
+        quantize("x", 0, *bb)
         quantize("x", 1, *bb)
-        product1(0, *bb, [6, 7], [1])
+        product1(0, *bb, [6, 7])
         product1(1, *bb, [0, 1])
         weave("V", "h", 0, *a)
-        weave("V", "x", 0, *c)
+        shared_weave("x", 0, 512, 640, 768)
         drain("S", 0, *bb)
-        quantize("h", 0, *a)
+        weave("V", "h", 1, *a)
         quantize("x", 0, *c)
         product1(0, *c, [2, 3], [0])
         weave("V", "x", 1, *c)
-        weave("V", "h", 1, *a)
+        quantize_both("h", 0)
         quantize("x", 1, *c)
         product1(0, *c, [2, 3], [1])
         product1(1, *c, [4, 5])
         drain("S", 1, *bb)
-        weave("S", "h", 0, 384, 512)
         weave("V", "x", 0, *d)
+        shared_weave("h", 0, 256, 384, 512)
         drain("S", 0, *c)
-        quantize("h", 1, *a)
         quantize("x", 0, *d)
         product1(0, *d, [6, 7], [0])
         weave("V", "x", 1, *d)
-        weave("V", "h", 0, 256, 384)
+        quantize("h", 0, *bb)
         quantize("x", 1, *d)
         drain("S", 1, *c)
         product1(0, *d, [6, 7], [1])
         product1(1, *d, [0, 1])
         weave("V", "h", 1, *bb)
-        quantize("h", 0, *bb)
-        y_banks(0, 512, [2, 3, 4, 5])
-        product2(0, *a, [0])
-        product2(0, *bb, [0])
-
-        v_sign("V", 1)
         drain("S", 0, *d)
+        weave("V", "h", 0, 512, 704)
         quantize("h", 1, *bb)
+        weave_signed(1, 0, 128)
         drain("S", 1, *d)
         weave("S", "h", 0, 704, 768)
-        weave("V", "v", 1, 0, 128)
+        y_banks(0, 512, [2, 3, 4, 5])
         for q in range(4):
             if q < 3:
-                weave("V", "v", 1, 128 * q + 128, 128 * q + 256)
+                weave_signed(1, 128 * q + 128, 128 * q + 256)
             else:
-                weave("V", "h", 0, 512, 704)
+                weave("V", "h", 1, *c)
             quantize("v", 1, 128 * q, 128 * q + 128)
-            product2(0, *a, [1], [q])
-            product2(0, *bb, [1], [q])
+            for g in range(2):
+                product2(0, *a, [g], [q])
+                product2(0, *bb, [g], [q])
         finish(0, 512, 1)
-        weave("V", "h", 1, *c)
         quantize("h", 0, *c)
         quantize("h", 1, *c)
         y_banks(*c, [6, 7])

@@ -19,6 +19,15 @@ PACK = 4
 PASS = P * PACK
 RUN = 4
 BANK = 512
+CHUNK = 256
+WARM_PASSES = 7
+
+W_SHARE = 352
+W_LAST_SHARE = 224
+X_FIRST_SHARE = 176
+X_GAP_SHARE = 128
+H_SECOND_SHARE = 128
+H_THIRD_SHARE = 192
 
 
 def tile_mix_kern_arc_gelu_kernel(tc, x, w, cw, cb, v, b, out):
@@ -31,158 +40,149 @@ def tile_mix_kern_arc_gelu_kernel(tc, x, w, cw, cb, v, b, out):
         def sb(name, shape, dtype):
             return keep.tile(shape, dtype, name=name, align_bytes=64)
 
-        hbm = {"w": w, "x": x, "v": v}
-        raw, woven, accs, rows, groups, codes, pairs = {}, {}, {}, {}, {}, {}, {}
+        def bank(name, number, shape):
+            return psum.tile(shape, F32, name=name, tag="bank%d" % number)
 
-        def load(kind, g, lo, hi):
-            tile = sb("%s_raw%d_%d" % (kind, g, lo), [P, PACK, hi - lo], F32)
-            nc.sync.dma_start(out=tile[:], in_=hbm[kind][g * PASS : (g + 1) * PASS, lo:hi].rearrange("(p s) c -> p s c", s=PACK))
-            raw.setdefault((kind, g), []).append((lo, hi, tile[:]))
+        slot_rows, woven, quantised = {}, {}, {}
+        both_passes, d_sums, y_sums, y_groups, v_raw, v_rows = {}, {}, {}, {}, {}, {}
 
         def find(table, key, lo, hi):
-            for a, z, ap in table[key]:
-                if a <= lo and hi <= z:
-                    return a, ap
+            for first, end, ap in table[key]:
+                if first <= lo and hi <= end:
+                    return first, ap
             raise ValueError("no tile holds these columns")
 
-        def block(kind, lo, hi):
+        def load(kind, hbm, g, lo, hi):
+            tile = sb("%s_raw%d_%d" % (kind, g, lo), [P, PACK, hi - lo], F32)
+            nc.sync.dma_start(out=tile[:], in_=hbm[g * PASS : (g + 1) * PASS, lo:hi].rearrange("(p s) c -> p s c", s=PACK))
+            slot_rows.setdefault((kind, g), []).append((lo, hi, tile[:]))
+
+        def load_v(g):
+            v_raw[g] = sb("v_raw%d" % g, [P, PACK, N], F32)
+            nc.sync.dma_start(out=v_raw[g][:], in_=v[g * PASS : (g + 1) * PASS, :].rearrange("(p s) c -> p s c", s=PACK))
+
+        def operand_tiles(kind, lo, hi):
             width = hi - lo
-            both = sb("%s_woven%d" % (kind, lo), [P, 2 * PACK * width], BF16)
+            values = sb("%s_woven%d" % (kind, lo), [P, 2 * PACK * width], BF16)
             words = sb("%s_codes%d" % (kind, lo), [P, 2 * width], U32)
-            planes = sb("%s_scales%d" % (kind, lo), [P, 2 * width], U8)
-            pairs[kind, lo] = (both, words, planes)
+            scales = sb("%s_scales%d" % (kind, lo), [P, 2 * width], U8)
+            both_passes[kind, lo] = (values, words, scales)
             for g in range(2):
-                woven.setdefault((kind, g), []).append((lo, hi, both[:, g * PACK * width : (g + 1) * PACK * width]))
                 cols = slice(g * width, (g + 1) * width)
-                codes.setdefault((kind, g), []).append((lo, hi, (words[:, cols], planes[:, cols])))
+                woven.setdefault((kind, g), []).append((lo, hi, values[:, g * PACK * width : (g + 1) * PACK * width]))
+                quantised.setdefault((kind, g), []).append((lo, hi, (words[:, cols], scales[:, cols])))
 
-        def row_tiles(kind, lo, hi):
+        def h_row_tiles(lo, hi):
             for g in range(2):
-                rows.setdefault((kind, g), []).append((lo, hi, sb("%s_rows%d_%d" % (kind, g, lo), [P, PACK, hi - lo], BF16)[:]))
+                slot_rows.setdefault(("h", g), []).append((lo, hi, sb("h_rows%d_%d" % (g, lo), [P, PACK, hi - lo], BF16)[:]))
 
-        def joint_rows(lo, hi):
-            width = hi - lo
-            pairs["rows", lo] = sb("h_rows_%d" % lo, [P, PACK, 2 * width], BF16)
-            for g in range(2):
-                rows.setdefault(("h", g), []).append((lo, hi, pairs["rows", lo][:, :, g * width : (g + 1) * width]))
-
-        def weave_h_both(lo):
-            dst = pairs["h", lo][0][:].rearrange("p (c i s) -> p c s i", i=RUN, s=PACK)
-            src = pairs["rows", lo][:].rearrange("p s (c i) -> p c s i", i=RUN)
-            nc.vector.tensor_scalar(out=dst, in0=src, scalar1=0.0, scalar2=None, op0=ALU.max)
-
-        def quantize_both(kind, lo):
-            both, words, planes = pairs[kind, lo]
-            nc.vector.quantize_mx(out=words[:].bitcast(FP8X4), scales=planes[:], in_=both[:])
-
-        def weave(engine, kind, g, lo, hi):
-            a, src = find(rows if (kind, g) in rows else raw, (kind, g), lo, hi)
-            src = src[:, :, lo - a : hi - a]
-            a, dst = find(woven, (kind, g), lo, hi)
+        def weave_views(kind, g, lo, hi):
+            first, src = find(slot_rows, (kind, g), lo, hi)
+            src = src[:, :, lo - first : hi - first]
+            first, dst = find(woven, (kind, g), lo, hi)
             if kind == "w":
-                dst = dst.rearrange("p (u m s) -> p m s u", u=PACK, s=PACK)[:, (lo - a) // PACK : (hi - a) // PACK]
-                src = src.rearrange("p s (m u) -> p m s u", u=PACK)
-            else:
-                dst = dst[:, PACK * (lo - a) : PACK * (hi - a)].rearrange("p (c i s) -> p c s i", i=RUN, s=PACK)
-                src = src.rearrange("p s (c i) -> p c s i", i=RUN)
-            if engine == "S":
-                nc.scalar.copy(out=dst, in_=src)
-            elif kind == "h":
+                dst = dst.rearrange("p (a e m s) -> p a m s e", a=2, e=2, s=PACK)[:, :, (lo - first) // PACK : (hi - first) // PACK]
+                return dst, src.rearrange("p s (m a e) -> p a m s e", a=2, e=2)
+            dst = dst[:, PACK * (lo - first) : PACK * (hi - first)].rearrange("p (c i s) -> p c s i", i=RUN, s=PACK)
+            return dst, src.rearrange("p s (c i) -> p c s i", i=RUN)
+
+        def weave(kind, g, lo, hi):
+            dst, src = weave_views(kind, g, lo, hi)
+            if kind == "h":
                 nc.vector.tensor_scalar(out=dst, in0=src, scalar1=0.0, scalar2=None, op0=ALU.max)
             else:
                 nc.vector.tensor_copy(out=dst, in_=src)
 
-        def shared_weave(kind, g, lo, cut, hi):
-            weave("S", kind, g, cut, hi)
-            weave("V", kind, g, lo, cut)
+        def signed_weave(lo, hi):
+            dst = both_passes["v", 0][0][:, PACK * (N + lo) : PACK * (N + hi)].rearrange("p (c i s) -> p c s i", i=RUN, s=PACK)
+            src = v_raw[1][:, :, lo:hi].rearrange("p s (c i) -> p c s i", i=RUN)
+            signs = sign[:, 1, :].unsqueeze(1).unsqueeze(3).to_broadcast([P, (hi - lo) // RUN, PACK, RUN])
+            nc.vector.tensor_tensor(out=dst, in0=src, in1=signs, op=ALU.mult)
+
+        def scalar_weave(kind, g, lo, hi):
+            dst, src = weave_views(kind, g, lo, hi)
+            nc.scalar.copy(out=dst, in_=src)
+
+        def shared_weave(kind, g, lo, hi, share):
+            scalar_weave(kind, g, lo + share, hi)
+            weave(kind, g, lo, lo + share)
 
         def operand(kind, g, lo, hi):
-            a, (words, planes) = find(codes, (kind, g), lo, hi)
-            return words[:, lo - a : hi - a].bitcast(FP8X4), planes[:, lo - a : hi - a]
+            first, (words, scales) = find(quantised, (kind, g), lo, hi)
+            return words[:, lo - first : hi - first].bitcast(FP8X4), scales[:, lo - first : hi - first]
 
         def quantize(kind, g, lo, hi):
-            a, src = find(woven, (kind, g), lo, hi)
-            words, planes = operand(kind, g, lo, hi)
-            nc.vector.quantize_mx(out=words, scales=planes, in_=src[:, PACK * (lo - a) : PACK * (hi - a)])
+            first, src = find(woven, (kind, g), lo, hi)
+            words, scales = operand(kind, g, lo, hi)
+            nc.vector.quantize_mx(out=words, scales=scales, in_=src[:, PACK * (lo - first) : PACK * (hi - first)])
 
-        def mx_pass(acc, stationary, cols, moving, g, lo, hi, first, last):
-            lhs, lhs_scale = operand(stationary, g, cols.start, cols.stop)
+        def quantize_both(kind, lo):
+            values, words, scales = both_passes[kind, lo]
+            nc.vector.quantize_mx(out=words[:].bitcast(FP8X4), scales=scales[:], in_=values[:])
+
+        def mx_pass(acc, stationary, col, moving, g, lo, hi, first, last):
+            lhs, lhs_scale = operand(stationary, g, col, col + P)
             rhs, rhs_scale = operand(moving, g, lo, hi)
             nc.tensor.matmul_mx(out=acc, lhsT=lhs, lhsT_scale=lhs_scale, rhs=rhs, rhs_scale=rhs_scale, start=first, stop=last)
 
-        def product1(jg, lo, hi, banks, passes=(0, 1), only=None):
+        def product1(half, lo, hi, banks, passes=(0, 1)):
             per = PACK // len(banks)
-            for n, bank in enumerate(banks):
-                if only is not None and n not in only:
-                    continue
+            for n, number in enumerate(banks):
                 if passes[0] == 0:
-                    tile = psum.tile([P, per, BANK // per], F32, name="d%d_%d_%d" % (jg, lo, n), tag="bank%d" % bank)
+                    tile = bank("d%d_%d_%d" % (half, lo, n), number, [P, per, BANK // per])
                     for m in range(per):
-                        accs["d", jg, lo, n * per + m] = tile[:, m, : hi - lo]
+                        d_sums[half, lo, n * per + m] = tile[:, m, : hi - lo]
                 for g in passes:
                     for m in range(per):
                         u = n * per + m
-                        cols = slice(jg * PASS + u * P, jg * PASS + (u + 1) * P)
-                        mx_pass(accs["d", jg, lo, u], "w", cols, "x", g, lo, hi, g == 0 and m == 0, g == 1 and m == per - 1)
+                        mx_pass(d_sums[half, lo, u], "w", half * PASS + u * P, "x", g, lo, hi, g == 0 and m == 0, g == 1 and m == per - 1)
 
-        def drain(engine, jg, lo, hi, slots=range(PACK)):
-            a, dst = find(rows, ("h", jg), lo, hi)
+        def drain(half, lo, hi, slots=range(PACK)):
+            first, dst = find(slot_rows, ("h", half), lo, hi)
             for u in slots:
-                src = accs["d", jg, lo, u]
-                if engine == "V":
-                    nc.vector.tensor_scalar(out=dst[:, u, lo - a : hi - a], in0=src, scalar1=gain[:, jg, u : u + 1],
-                                            scalar2=shift[:, jg, u : u + 1], op0=ALU.mult, op1=ALU.add)
-                else:
-                    nc.scalar.activation(out=dst[:, u, lo - a : hi - a], in_=src, func=ACT.Relu,
-                                         bias=shift[:, jg, u : u + 1], scale=gain[:, jg, u : u + 1])
+                nc.scalar.activation(out=dst[:, u, :], in_=d_sums[half, lo, u], func=ACT.Relu,
+                                     bias=shift[:, half, u : u + 1], scale=gain[:, half, u : u + 1])
 
-        def v_sign(engine, g, slots=range(PACK)):
-            a, src = find(raw, ("v", g), 0, N)
-            c, dst = find(rows, ("v", g), 0, N)
+        def vector_drain(half, lo, hi, slots):
+            first, dst = find(slot_rows, ("h", half), lo, hi)
+            for u in slots:
+                nc.vector.tensor_scalar(out=dst[:, u, :], in0=d_sums[half, lo, u], scalar1=gain[:, half, u : u + 1],
+                                        scalar2=shift[:, half, u : u + 1], op0=ALU.mult, op1=ALU.add)
+
+        def sign_rows(g, slots):
             for s in slots:
-                if engine == "S":
-                    nc.scalar.activation(out=dst[:, s, :], in_=src[:, s, :], func=ACT.Copy, scale=sign[:, g, s : s + 1])
-                else:
-                    nc.vector.tensor_scalar(out=dst[:, s, :], in0=src[:, s, :], scalar1=sign[:, g, s : s + 1], scalar2=None, op0=ALU.mult)
+                nc.vector.tensor_scalar(out=v_rows[g][:, s, :], in0=v_raw[g][:, s, :], scalar1=sign[:, g, s : s + 1], scalar2=None, op0=ALU.mult)
 
-        def weave_signed(g, lo, hi):
-            a, src = find(raw, ("v", g), lo, hi)
-            c, dst = find(woven, ("v", g), lo, hi)
-            dst = dst[:, PACK * (lo - c) : PACK * (hi - c)].rearrange("p (c i s) -> p c s i", i=RUN, s=PACK)
-            src = src[:, :, lo - a : hi - a].rearrange("p s (c i) -> p c s i", i=RUN)
-            signs = sign_run[:, g, :, :].unsqueeze(1).to_broadcast([P, (hi - lo) // RUN, PACK, RUN])
-            nc.vector.tensor_tensor(out=dst, in0=src, in1=signs, op=ALU.mult)
+        def scalar_sign_rows(g, slots):
+            for s in slots:
+                nc.scalar.activation(out=v_rows[g][:, s, :], in_=v_raw[g][:, s, :], func=ACT.Copy, scale=sign[:, g, s : s + 1])
 
         def y_banks(lo, hi, banks):
             per = PACK // len(banks)
-            for n, bank in enumerate(banks):
-                tile = psum.tile([P, per, BANK // per], F32, name="y%d_%d" % (lo, n), tag="bank%d" % bank)
-                group = {"left": 2 * per * (hi - lo), "open": False}
+            for n, number in enumerate(banks):
+                tile = bank("y%d_%d" % (lo, n), number, [P, per, BANK // per])
+                group = {"columns left": 2 * per * (hi - lo), "open": False}
                 for m in range(per):
-                    accs["y", n * per + m, lo] = tile[:, m, : hi - lo]
-                    groups[n * per + m, lo] = group
+                    y_sums[n * per + m, lo] = tile[:, m, : hi - lo]
+                    y_groups[n * per + m, lo] = group
 
-        def product2(base, lo, hi, passes=(0, 1), tiles=range(PACK)):
+        def product2(base, lo, hi, g, tiles):
             for q in tiles:
-                for g in passes:
-                    group = groups[q, base]
-                    group["left"] = group["left"] - (hi - lo)
-                    mx_pass(accs["y", q, base][:, lo - base : hi - base], "v", slice(q * P, (q + 1) * P), "h", g, lo, hi,
-                            not group["open"], group["left"] == 0)
-                    group["open"] = True
+                group = y_groups[q, base]
+                group["columns left"] = group["columns left"] - (hi - lo)
+                mx_pass(y_sums[q, base][:, lo - base : hi - base], "v", q * P, "h", g, lo, hi,
+                        not group["open"], group["columns left"] == 0)
+                group["open"] = True
 
-        def finish(lo, hi, group=1, tiles=range(PACK)):
-            for n, q in enumerate(tiles):
-                if n % group == 0:
-                    res = sb("y_sb%d_%d" % (q, lo), [P, group, hi - lo], F32)
-                nc.scalar.activation(out=res[:, n % group, :], in_=accs["y", q, lo], func=ACT.Gelu_apprx_tanh, bias=b_sb[:, q : q + 1])
-                if n % group == group - 1:
-                    nc.sync.dma_start(out=out.rearrange("(q p) t -> p q t", p=P)[:, q + 1 - group : q + 1, lo:hi], in_=res[:])
+        def finish(lo, hi):
+            for q in range(N // P):
+                res = sb("y_sb%d_%d" % (q, lo), [P, hi - lo], F32)
+                nc.scalar.activation(out=res[:], in_=y_sums[q, lo], func=ACT.Gelu_apprx_tanh, bias=b_sb[:, q : q + 1])
+                nc.sync.dma_start(out=out[q * P : (q + 1) * P, lo:hi], in_=res[:])
 
         cb_sb = sb("cb_sb", [P, 2, PACK], F32)
-        b_sb = sb("b_sb", [P, PACK], F32)
+        b_sb = sb("b_sb", [P, N // P], F32)
         sign = sb("sign", [P, 2, PACK], F32)
-        sign_run = sb("sign_run", [P, 2, PACK, RUN], F32)
         gain = sb("gain", [P, 2, PACK], F32)
         shift = sb("shift", [P, 2, PACK], F32)
         stage = sb("stage", [P, PASS], F32)
@@ -194,150 +194,159 @@ def tile_mix_kern_arc_gelu_kernel(tc, x, w, cw, cb, v, b, out):
             nc.sync.dma_start(out=stage[4:8, 0:P], in_=b.rearrange("(q p) -> q p", p=P))
 
         def turn_vectors():
-            turned = psum.tile([P, PACK, P], F32, name="turned", tag="bank6")
-            turned_b = psum.tile([P, P], F32, name="turned_b", tag="bank7")
+            turned = bank("turned", 6, [P, PACK, P])
+            turned_b = bank("turned_b", 7, [P, P])
             for slot in range(PACK):
                 nc.tensor.transpose(turned[:, slot, :], stage[:, slot::PACK], ident[:])
             nc.tensor.transpose(turned_b[:], stage[:, 0:P], ident[:])
             nc.scalar.activation(out=gain[:], in_=turned[:, :, 0:2].rearrange("p s g -> p g s"), func=ACT.Abs)
             nc.scalar.activation(out=sign[:], in_=turned[:, :, 0:2].rearrange("p s g -> p g s"), func=ACT.Sign)
             nc.scalar.copy(out=cb_sb[:], in_=turned[:, :, 2:4].rearrange("p s g -> p g s"))
-            nc.scalar.copy(out=b_sb[:], in_=turned_b[:, 4:8])
+            return turned_b
 
-        def scaled_offsets():
+        def derive_constants():
             nc.vector.tensor_tensor(out=shift[:], in0=cb_sb[:], in1=gain[:], op=ALU.mult)
-            nc.vector.tensor_copy(out=sign_run[:], in_=sign[:].unsqueeze(3).to_broadcast([P, 2, PACK, RUN]))
 
         def warm_table():
             warm = sb("warm", [P, 1], F32)
             nc.scalar.activation(out=warm[:], in_=ident[:, 0:1], func=ACT.Gelu_apprx_tanh)
 
         def warm_operand():
-            ones = sb("warm_values", [P, PACK * 256], BF16)
-            nc.gpsimd.memset(ones[:], 1.0)
-            block_tiles = (ones, sb("warm_codes", [P, 256], U32), sb("warm_scales", [P, 256], U8))
-            pairs["warm", 0] = block_tiles
+            words = sb("warm_codes", [P, CHUNK], U32)
+            scales = sb("warm_scales", [P, CHUNK], U8)
+            nc.vector.quantize_mx(out=words[:].bitcast(FP8X4), scales=scales[:], in_=ones[:])
+            return words, scales
 
-        def warm_array(count, bank):
-            quantize_both("warm", 0)
-            ones, words, planes = pairs["warm", 0]
-            sink = psum.tile([P, 256], F32, name="warm_sink", tag="bank%d" % bank)
-            for n in range(count):
-                nc.tensor.matmul_mx(out=sink[:], lhsT=words[:, 0:P].bitcast(FP8X4), lhsT_scale=planes[:, 0:P],
-                                    rhs=words[:].bitcast(FP8X4), rhs_scale=planes[:], start=True, stop=True)
+        def warm_array(words, scales):
+            sink = bank("warm_sink", 7, [P, CHUNK])
+            for n in range(WARM_PASSES):
+                nc.tensor.matmul_mx(out=sink[:], lhsT=words[:, 0:P].bitcast(FP8X4), lhsT_scale=scales[:, 0:P],
+                                    rhs=words[:].bitcast(FP8X4), rhs_scale=scales[:], start=True, stop=True)
+
+        chunks = [(lo, lo + CHUNK) for lo in range(0, T, CHUNK)]
+        c0, c1, c2, c3 = chunks
+        halves = [(0, PASS), (PASS, J)]
+        tiles = [(q * P, (q + 1) * P) for q in range(N // P)]
 
         nc.vector.memset(stage[:], 0.0)
         make_identity(nc, ident[:])
-
-        a, bb, c, d = (0, 256), (256, 512), (512, 768), (768, 1024)
-        load("w", 0, 0, 1024)
+        load("w", w, 0, 0, J)
         load_vectors()
-        load("v", 0, 0, 512)
-        load("w", 1, 0, 1024)
-        for lo, hi in (a, bb, c, d):
-            load("x", 0, lo, hi)
-            load("x", 1, lo, hi)
-        load("v", 1, 0, 512)
-
+        load_v(0)
+        load("w", w, 1, 0, J)
+        for lo, hi in chunks:
+            load("x", x, 0, lo, hi)
+            load("x", x, 1, lo, hi)
+        load_v(1)
         warm_table()
-        warm_operand()
-        for lo, hi in (a, bb, c, d):
-            block("x", lo, hi)
-            block("h", lo, hi)
-            row_tiles("h", lo, hi)
-        for lo in (0, 512):
-            block("w", lo, lo + 512)
-        block("v", 0, 512)
-        row_tiles("v", 0, 512)
-        for lo in (0, 512):
-            shared_weave("w", 0, lo, lo + 352, lo + 512)
-        turn_vectors()
-        for lo in (0, 512):
-            quantize("w", 0, lo, lo + 512)
-        scaled_offsets()
+        ones = sb("warm_values", [P, PACK * CHUNK], BF16)
+        nc.gpsimd.memset(ones[:], 1.0)
+        for lo, hi in chunks:
+            operand_tiles("x", lo, hi)
+            operand_tiles("h", lo, hi)
+            h_row_tiles(lo, hi)
+        for lo, hi in halves:
+            operand_tiles("w", lo, hi)
+        operand_tiles("v", 0, N)
+        v_rows[0] = sb("v_rows0", [P, PACK, N], BF16)
+        slot_rows["v", 0] = [(0, N, v_rows[0][:])]
 
-        v_sign("S", 0, [3])
-        v_sign("V", 0, [0, 1, 2])
-        shared_weave("v", 0, 0, 352, 512)
-        quantize("v", 0, 0, 512)
-        warm_array(8, 7)
+        for lo, hi in halves:
+            shared_weave("w", 0, lo, hi, W_SHARE)
+        turned_b = turn_vectors()
+        for lo, hi in halves:
+            quantize("w", 0, lo, hi)
+        derive_constants()
+        scalar_sign_rows(0, [3])
+        sign_rows(0, [0, 1, 2])
+        shared_weave("v", 0, 0, N, W_SHARE)
+        quantize("v", 0, 0, N)
+        warm_words, warm_scales = warm_operand()
 
-        shared_weave("w", 1, 0, 352, 512)
-        shared_weave("w", 1, 512, 736, 1024)
-        weave("V", "x", 0, *a)
-        quantize("w", 1, 0, 512)
-        quantize("x", 0, *a)
-        product1(0, *a, [0, 1, 2, 3], [0])
-        product1(1, *a, [4, 5], [0])
-        shared_weave("x", 1, 0, 176, 256)
-        quantize("w", 1, 512, 768)
-        quantize("x", 1, *a)
-        product1(0, *a, [0, 1, 2, 3], [1])
-        quantize("w", 1, 768, 1024)
-        product1(1, *a, [4, 5], [1])
-        shared_weave("x", 0, 256, 368, 512)
-        drain("V", 0, *a, [0, 1])
-        drain("S", 0, *a, [2, 3])
-        weave("V", "x", 1, *bb)
-        drain("S", 1, *a)
-        quantize("x", 0, *bb)
-        quantize("x", 1, *bb)
-        product1(0, *bb, [6, 7])
-        product1(1, *bb, [0, 1])
-        weave("V", "h", 0, *a)
-        shared_weave("x", 0, 512, 640, 768)
-        drain("S", 0, *bb)
-        weave("V", "h", 1, *a)
-        quantize("x", 0, *c)
-        product1(0, *c, [2, 3], [0])
-        weave("V", "x", 1, *c)
-        quantize_both("h", 0)
-        quantize("x", 1, *c)
-        product1(0, *c, [2, 3], [1])
-        product1(1, *c, [4, 5])
-        drain("S", 1, *bb)
-        weave("V", "x", 0, *d)
-        shared_weave("h", 0, 256, 384, 512)
-        drain("S", 0, *c)
-        quantize("x", 0, *d)
-        product1(0, *d, [6, 7], [0])
-        weave("V", "x", 1, *d)
-        quantize("h", 0, *bb)
-        quantize("x", 1, *d)
-        drain("S", 1, *c)
-        product1(0, *d, [6, 7], [1])
-        product1(1, *d, [0, 1])
-        weave("V", "h", 1, *bb)
-        drain("S", 0, *d)
-        weave("V", "h", 0, 512, 704)
-        quantize("h", 1, *bb)
-        weave_signed(1, 0, 128)
-        drain("S", 1, *d)
-        weave("S", "h", 0, 704, 768)
-        y_banks(0, 512, [2, 3, 4, 5])
-        for q in range(4):
-            if q < 3:
-                weave_signed(1, 128 * q + 128, 128 * q + 256)
+        shared_weave("w", 1, *halves[0], W_SHARE)
+        nc.scalar.copy(out=b_sb[:], in_=turned_b[:, 4:8])
+        warm_array(warm_words, warm_scales)
+        shared_weave("w", 1, *halves[1], W_LAST_SHARE)
+        weave("x", 0, *c0)
+        quantize("w", 1, *halves[0])
+        quantize("x", 0, *c0)
+        product1(0, *c0, [0, 1, 2, 3], [0])
+        shared_weave("x", 1, *c0, X_FIRST_SHARE)
+        quantize("w", 1, PASS, PASS + 2 * P)
+        quantize("x", 1, *c0)
+        product1(0, *c0, [0, 1, 2, 3], [1])
+        quantize("w", 1, PASS + 2 * P, J)
+        product1(1, *c0, [4, 5])
+
+        shared_weave("x", 0, *c1, X_GAP_SHARE)
+        vector_drain(0, *c0, [0, 1])
+        drain(0, *c0, [2, 3])
+        weave("x", 1, *c1)
+        drain(1, *c0)
+        quantize("x", 0, *c1)
+        quantize("x", 1, *c1)
+        product1(0, *c1, [6, 7])
+        product1(1, *c1, [0, 1])
+
+        weave("h", 0, *c0)
+        shared_weave("x", 0, *c2, X_GAP_SHARE)
+        drain(0, *c1)
+        weave("h", 1, *c0)
+        quantize("x", 0, *c2)
+        product1(0, *c2, [2, 3], [0])
+        weave("x", 1, *c2)
+        quantize_both("h", c0[0])
+        quantize("x", 1, *c2)
+        product1(0, *c2, [2, 3], [1])
+        product1(1, *c2, [4, 5])
+        drain(1, *c1)
+
+        weave("x", 0, *c3)
+        shared_weave("h", 0, *c1, H_SECOND_SHARE)
+        drain(0, *c2)
+        quantize("x", 0, *c3)
+        product1(0, *c3, [6, 7], [0])
+        weave("x", 1, *c3)
+        quantize("h", 0, *c1)
+        quantize("x", 1, *c3)
+        drain(1, *c2)
+        product1(0, *c3, [6, 7], [1])
+        product1(1, *c3, [0, 1])
+        weave("h", 1, *c1)
+        drain(0, *c3)
+        weave("h", 0, c2[0], c2[0] + H_THIRD_SHARE)
+        quantize("h", 1, *c1)
+
+        signed_weave(*tiles[0])
+        drain(1, *c3)
+        scalar_weave("h", 0, c2[0] + H_THIRD_SHARE, c2[1])
+        y_banks(c0[0], c1[1], [2, 3, 4, 5])
+        for q, (lo, hi) in enumerate(tiles):
+            if q + 1 < len(tiles):
+                signed_weave(*tiles[q + 1])
             else:
-                weave("V", "h", 1, *c)
-            quantize("v", 1, 128 * q, 128 * q + 128)
+                weave("h", 1, *c2)
+            quantize("v", 1, lo, hi)
             for g in range(2):
-                product2(0, *a, [g], [q])
-                product2(0, *bb, [g], [q])
-        finish(0, 512, 1)
-        quantize("h", 0, *c)
-        quantize("h", 1, *c)
-        y_banks(*c, [6, 7])
+                product2(c0[0], *c0, g, [q])
+                product2(c0[0], *c1, g, [q])
+        finish(c0[0], c1[1])
+
+        quantize("h", 0, *c2)
+        quantize("h", 1, *c2)
+        y_banks(*c2, [6, 7])
         for pair in ([0, 1], [2, 3]):
-            product2(512, *c, [0], pair)
-            product2(512, *c, [1], pair)
-        weave("V", "h", 0, *d)
-        weave("V", "h", 1, *d)
-        finish(*c, 1)
-        quantize("h", 0, *d)
-        y_banks(*d, [0, 1, 2, 3])
-        product2(768, *d, [0], [0, 1])
-        quantize("h", 1, *d)
-        product2(768, *d, [1], [0, 1])
-        product2(768, *d, [0, 1], [2, 3])
-        finish(*d, 1)
+            for g in range(2):
+                product2(c2[0], *c2, g, pair)
+        weave("h", 0, *c3)
+        weave("h", 1, *c3)
+        finish(*c2)
+        quantize("h", 0, *c3)
+        y_banks(*c3, [0, 1, 2, 3])
+        product2(c3[0], *c3, 0, [0, 1])
+        quantize("h", 1, *c3)
+        product2(c3[0], *c3, 1, [0, 1])
+        for q in (2, 3):
+            for g in range(2):
+                product2(c3[0], *c3, g, [q])
+        finish(*c3)

@@ -24,9 +24,10 @@ WARM_PASSES = 7
 
 W_SHARE = 352
 W_LAST_SHARE = 224
-X_FIRST_SHARE = 176
+X_FIRST_SHARE = 192
 X_GAP_SHARE = 128
-H_SECOND_SHARE = 128
+X_THIRD_SHARE = 64
+X_LAST_SHARE = 144
 H_THIRD_SHARE = 192
 
 
@@ -116,10 +117,6 @@ def tile_mix_kern_arc_gelu_kernel(tc, x, w, cw, cb, v, b, out):
             words, scales = operand(kind, g, lo, hi)
             nc.vector.quantize_mx(out=words, scales=scales, in_=src[:, PACK * (lo - first) : PACK * (hi - first)])
 
-        def quantize_both(kind, lo):
-            values, words, scales = both_passes[kind, lo]
-            nc.vector.quantize_mx(out=words[:].bitcast(FP8X4), scales=scales[:], in_=values[:])
-
         def mx_pass(acc, stationary, col, moving, g, lo, hi, first, last):
             lhs, lhs_scale = operand(stationary, g, col, col + P)
             rhs, rhs_scale = operand(moving, g, lo, hi)
@@ -174,8 +171,8 @@ def tile_mix_kern_arc_gelu_kernel(tc, x, w, cw, cb, v, b, out):
                         not group["open"], group["columns left"] == 0)
                 group["open"] = True
 
-        def finish(lo, hi):
-            for q in range(N // P):
+        def finish(lo, hi, tiles=range(N // P)):
+            for q in tiles:
                 res = sb("y_sb%d_%d" % (q, lo), [P, hi - lo], F32)
                 nc.scalar.activation(out=res[:], in_=y_sums[q, lo], func=ACT.Gelu_apprx_tanh, bias=b_sb[:, q : q + 1])
                 nc.sync.dma_start(out=out[q * P : (q + 1) * P, lo:hi], in_=res[:])
@@ -257,9 +254,9 @@ def tile_mix_kern_arc_gelu_kernel(tc, x, w, cw, cb, v, b, out):
         for lo, hi in halves:
             quantize("w", 0, lo, hi)
         derive_constants()
-        scalar_sign_rows(0, [3])
-        sign_rows(0, [0, 1, 2])
-        shared_weave("v", 0, 0, N, W_SHARE)
+        scalar_sign_rows(0, [2, 3])
+        sign_rows(0, [0, 1])
+        weave("v", 0, 0, N)
         quantize("v", 0, 0, N)
         warm_words, warm_scales = warm_operand()
 
@@ -268,69 +265,76 @@ def tile_mix_kern_arc_gelu_kernel(tc, x, w, cw, cb, v, b, out):
         warm_array(warm_words, warm_scales)
         shared_weave("w", 1, *halves[1], W_LAST_SHARE)
         weave("x", 0, *c0)
-        quantize("w", 1, *halves[0])
+        quantize("w", 1, 0, 2 * P)
         quantize("x", 0, *c0)
         product1(0, *c0, [0, 1, 2, 3], [0])
         shared_weave("x", 1, *c0, X_FIRST_SHARE)
-        quantize("w", 1, PASS, PASS + 2 * P)
+        quantize("w", 1, 2 * P, PASS)
         quantize("x", 1, *c0)
         product1(0, *c0, [0, 1, 2, 3], [1])
-        quantize("w", 1, PASS + 2 * P, J)
+        quantize("w", 1, *halves[1])
         product1(1, *c0, [4, 5])
 
         shared_weave("x", 0, *c1, X_GAP_SHARE)
         vector_drain(0, *c0, [0, 1])
         drain(0, *c0, [2, 3])
+        quantize("x", 0, *c1)
+        product1(0, *c1, [6, 7], [0])
         weave("x", 1, *c1)
         drain(1, *c0)
-        quantize("x", 0, *c1)
+        weave("h", 0, *c0)
         quantize("x", 1, *c1)
-        product1(0, *c1, [6, 7])
+        product1(0, *c1, [6, 7], [1])
         product1(1, *c1, [0, 1])
 
-        weave("h", 0, *c0)
-        shared_weave("x", 0, *c2, X_GAP_SHARE)
+        shared_weave("x", 0, *c2, X_THIRD_SHARE)
         drain(0, *c1)
         weave("h", 1, *c0)
+        quantize("h", 0, *c0)
+        weave("x", 1, *c2)
         quantize("x", 0, *c2)
         product1(0, *c2, [2, 3], [0])
-        weave("x", 1, *c2)
-        quantize_both("h", c0[0])
         quantize("x", 1, *c2)
         product1(0, *c2, [2, 3], [1])
+        quantize("h", 1, *c0)
         product1(1, *c2, [4, 5])
         drain(1, *c1)
 
-        weave("x", 0, *c3)
-        shared_weave("h", 0, *c1, H_SECOND_SHARE)
+        weave("h", 0, *c1)
+        shared_weave("x", 0, *c3, X_LAST_SHARE)
         drain(0, *c2)
+        quantize("h", 0, *c1)
+        weave("x", 1, *c3)
         quantize("x", 0, *c3)
         product1(0, *c3, [6, 7], [0])
-        weave("x", 1, *c3)
-        quantize("h", 0, *c1)
         quantize("x", 1, *c3)
         drain(1, *c2)
         product1(0, *c3, [6, 7], [1])
         product1(1, *c3, [0, 1])
         weave("h", 1, *c1)
+        shared_weave("h", 0, *c2, H_THIRD_SHARE)
         drain(0, *c3)
-        weave("h", 0, c2[0], c2[0] + H_THIRD_SHARE)
-        quantize("h", 1, *c1)
 
         signed_weave(*tiles[0])
-        drain(1, *c3)
-        scalar_weave("h", 0, c2[0] + H_THIRD_SHARE, c2[1])
+        quantize("h", 1, *c1)
         y_banks(c0[0], c1[1], [2, 3, 4, 5])
         for q, (lo, hi) in enumerate(tiles):
-            if q + 1 < len(tiles):
-                signed_weave(*tiles[q + 1])
-            else:
+            if q + 1 == len(tiles):
                 weave("h", 1, *c2)
+            elif q > 0:
+                signed_weave(*tiles[q + 1])
             quantize("v", 1, lo, hi)
+            if q == 0:
+                signed_weave(*tiles[1])
             for g in range(2):
                 product2(c0[0], *c0, g, [q])
                 product2(c0[0], *c1, g, [q])
-        finish(c0[0], c1[1])
+        drain(1, *c3, [0, 1])
+        finish(c0[0], c1[1], [0])
+        drain(1, *c3, [2])
+        finish(c0[0], c1[1], [1])
+        drain(1, *c3, [3])
+        finish(c0[0], c1[1], [2, 3])
 
         quantize("h", 0, *c2)
         quantize("h", 1, *c2)

@@ -22,6 +22,10 @@ BANK = 512
 CHUNK = 256
 WARM_PASSES = 7
 
+CW_ROWS = slice(0, P, 64)
+CB_ROWS = slice(4, P, 64)
+B_ROWS = slice(8, P, 32)
+
 W_SHARE = 352
 W_LAST_SHARE = 224
 X_FIRST_SHARE = 192
@@ -186,9 +190,9 @@ def tile_mix_kern_arc_gelu_kernel(tc, x, w, cw, cb, v, b, out):
         ident = sb("ident", [P, P], F32)
 
         def load_vectors():
-            nc.sync.dma_start(out=stage[0:2, :], in_=cw.rearrange("(g c) -> g c", g=2))
-            nc.sync.dma_start(out=stage[2:4, :], in_=cb.rearrange("(g c) -> g c", g=2))
-            nc.sync.dma_start(out=stage[4:8, 0:P], in_=b.rearrange("(q p) -> q p", p=P))
+            nc.sync.dma_start(out=stage[CW_ROWS, :], in_=cw.rearrange("(g c) -> g c", g=2))
+            nc.sync.dma_start(out=stage[CB_ROWS, :], in_=cb.rearrange("(g c) -> g c", g=2))
+            nc.sync.dma_start(out=stage[B_ROWS, 0:P], in_=b.rearrange("(q p) -> q p", p=P))
 
         def turn_vectors():
             turned = bank("turned", 6, [P, PACK, P])
@@ -196,9 +200,9 @@ def tile_mix_kern_arc_gelu_kernel(tc, x, w, cw, cb, v, b, out):
             for slot in range(PACK):
                 nc.tensor.transpose(turned[:, slot, :], stage[:, slot::PACK], ident[:])
             nc.tensor.transpose(turned_b[:], stage[:, 0:P], ident[:])
-            nc.scalar.activation(out=gain[:], in_=turned[:, :, 0:2].rearrange("p s g -> p g s"), func=ACT.Abs)
-            nc.scalar.activation(out=sign[:], in_=turned[:, :, 0:2].rearrange("p s g -> p g s"), func=ACT.Sign)
-            nc.scalar.copy(out=cb_sb[:], in_=turned[:, :, 2:4].rearrange("p s g -> p g s"))
+            nc.scalar.activation(out=gain[:], in_=turned[:, :, CW_ROWS].rearrange("p s g -> p g s"), func=ACT.Abs)
+            nc.scalar.activation(out=sign[:], in_=turned[:, :, CW_ROWS].rearrange("p s g -> p g s"), func=ACT.Sign)
+            nc.scalar.copy(out=cb_sb[:], in_=turned[:, :, CB_ROWS].rearrange("p s g -> p g s"))
             return turned_b
 
         def derive_constants():
@@ -261,7 +265,7 @@ def tile_mix_kern_arc_gelu_kernel(tc, x, w, cw, cb, v, b, out):
         warm_words, warm_scales = warm_operand()
 
         shared_weave("w", 1, *halves[0], W_SHARE)
-        nc.scalar.copy(out=b_sb[:], in_=turned_b[:, 4:8])
+        nc.scalar.copy(out=b_sb[:], in_=turned_b[:, B_ROWS])
         warm_array(warm_words, warm_scales)
         shared_weave("w", 1, *halves[1], W_LAST_SHARE)
         weave("x", 0, *c0)

from contextlib import ExitStack

import concourse.mybir as mybir
from concourse.masks import make_identity

K, J, N, T = 1024, 1024, 512, 1024
FLOPS = 2 * K * J * T + 2 * J * N * T

F32 = mybir.dt.float32
BF16 = mybir.dt.bfloat16
U32 = mybir.dt.uint32
U8 = mybir.dt.uint8
FP8X4 = mybir.dt.float8_e4m3fn_x4
ALU = mybir.AluOpType
ACT = mybir.ActivationFunctionType

P = 128
PACK = 4
PASS = P * PACK
RUN = 4
BANK = 512
CHUNK = 256
WARM_PASSES = 7

CW_ROWS = slice(0, P, 64)
CB_ROWS = slice(4, P, 64)
B_ROWS = slice(8, P, 32)

W_SHARE = 352
W_LAST_SHARE = 224
X_FIRST_SHARE = 192
X_GAP_SHARE = 128
X_THIRD_SHARE = 64
X_LAST_SHARE = 144
H_THIRD_SHARE = 192


def tile_mix_kern_arc_gelu_kernel(tc, x, w, cw, cb, v, b, out):
    nc = tc.nc
    with ExitStack() as ctx:
        keep = ctx.enter_context(tc.tile_pool(name="keep", bufs=1))
        psum = ctx.enter_context(tc.psum_pool(name="psum", bufs=1))
        ctx.enter_context(tc.manual_schedule())

        def sb(name, shape, dtype):
            return keep.tile(shape, dtype, name=name, align_bytes=64)

        def bank(name, number, shape):
            return psum.tile(shape, F32, name=name, tag="bank%d" % number)

        slot_rows, woven, quantised = {}, {}, {}
        both_passes, d_sums, y_sums, y_groups, v_raw, v_rows = {}, {}, {}, {}, {}, {}

        def find(table, key, lo, hi):
            for first, end, ap in table[key]:
                if first <= lo and hi <= end:
                    return first, ap
            raise ValueError("no tile holds these columns")

        def load(kind, hbm, g, lo, hi):
            tile = sb("%s_raw%d_%d" % (kind, g, lo), [P, PACK, hi - lo], F32)
            nc.sync.dma_start(out=tile[:], in_=hbm[g * PASS : (g + 1) * PASS, lo:hi].rearrange("(p s) c -> p s c", s=PACK))
            slot_rows.setdefault((kind, g), []).append((lo, hi, tile[:]))

        def load_v(g):
            v_raw[g] = sb("v_raw%d" % g, [P, PACK, N], F32)
            nc.sync.dma_start(out=v_raw[g][:], in_=v[g * PASS : (g + 1) * PASS, :].rearrange("(p s) c -> p s c", s=PACK))

        def operand_tiles(kind, lo, hi):
            width = hi - lo
            values = sb("%s_woven%d" % (kind, lo), [P, 2 * PACK * width], BF16)
            words = sb("%s_codes%d" % (kind, lo), [P, 2 * width], U32)
            scales = sb("%s_scales%d" % (kind, lo), [P, 2 * width], U8)
            both_passes[kind, lo] = (values, words, scales)
            for g in range(2):
                cols = slice(g * width, (g + 1) * width)
                woven.setdefault((kind, g), []).append((lo, hi, values[:, g * PACK * width : (g + 1) * PACK * width]))
                quantised.setdefault((kind, g), []).append((lo, hi, (words[:, cols], scales[:, cols])))

        def h_row_tiles(lo, hi):
            for g in range(2):
                slot_rows.setdefault(("h", g), []).append((lo, hi, sb("h_rows%d_%d" % (g, lo), [P, PACK, hi - lo], BF16)[:]))

        def weave_views(kind, g, lo, hi):
            first, src = find(slot_rows, (kind, g), lo, hi)
            src = src[:, :, lo - first : hi - first]
            first, dst = find(woven, (kind, g), lo, hi)
            if kind == "w":
                dst = dst.rearrange("p (a e m s) -> p a m s e", a=2, e=2, s=PACK)[:, :, (lo - first) // PACK : (hi - first) // PACK]
                return dst, src.rearrange("p s (m a e) -> p a m s e", a=2, e=2)
            dst = dst[:, PACK * (lo - first) : PACK * (hi - first)].rearrange("p (c i s) -> p c s i", i=RUN, s=PACK)
            return dst, src.rearrange("p s (c i) -> p c s i", i=RUN)

        def weave(kind, g, lo, hi):
            dst, src = weave_views(kind, g, lo, hi)
            if kind == "h":
                nc.vector.tensor_scalar(out=dst, in0=src, scalar1=0.0, scalar2=None, op0=ALU.max)
            else:
                nc.vector.tensor_copy(out=dst, in_=src)

        def signed_weave(lo, hi):
            dst = both_passes["v", 0][0][:, PACK * (N + lo) : PACK * (N + hi)].rearrange("p (c i s) -> p c s i", i=RUN, s=PACK)
            src = v_raw[1][:, :, lo:hi].rearrange("p s (c i) -> p c s i", i=RUN)
            signs = sign[:, 1, :].unsqueeze(1).unsqueeze(3).to_broadcast([P, (hi - lo) // RUN, PACK, RUN])
            nc.vector.tensor_tensor(out=dst, in0=src, in1=signs, op=ALU.mult)

        def scalar_weave(kind, g, lo, hi):
            dst, src = weave_views(kind, g, lo, hi)
            nc.scalar.copy(out=dst, in_=src)

        def shared_weave(kind, g, lo, hi, share):
            scalar_weave(kind, g, lo + share, hi)
            weave(kind, g, lo, lo + share)

        def operand(kind, g, lo, hi):
            first, (words, scales) = find(quantised, (kind, g), lo, hi)
            return words[:, lo - first : hi - first].bitcast(FP8X4), scales[:, lo - first : hi - first]

        def quantize(kind, g, lo, hi):
            first, src = find(woven, (kind, g), lo, hi)
            words, scales = operand(kind, g, lo, hi)
            nc.vector.quantize_mx(out=words, scales=scales, in_=src[:, PACK * (lo - first) : PACK * (hi - first)])

        def mx_pass(acc, stationary, col, moving, g, lo, hi, first, last):
            lhs, lhs_scale = operand(stationary, g, col, col + P)
            rhs, rhs_scale = operand(moving, g, lo, hi)
            nc.tensor.matmul_mx(out=acc, lhsT=lhs, lhsT_scale=lhs_scale, rhs=rhs, rhs_scale=rhs_scale, start=first, stop=last)

        def product1(half, lo, hi, banks, passes=(0, 1)):
            per = PACK // len(banks)
            for n, number in enumerate(banks):
                if passes[0] == 0:
                    tile = bank("d%d_%d_%d" % (half, lo, n), number, [P, per, BANK // per])
                    for m in range(per):
                        d_sums[half, lo, n * per + m] = tile[:, m, : hi - lo]
                for g in passes:
                    for m in range(per):
                        u = n * per + m
                        mx_pass(d_sums[half, lo, u], "w", half * PASS + u * P, "x", g, lo, hi, g == 0 and m == 0, g == 1 and m == per - 1)

        def drain(half, lo, hi, slots=range(PACK)):
            first, dst = find(slot_rows, ("h", half), lo, hi)
            for u in slots:
                nc.scalar.activation(out=dst[:, u, :], in_=d_sums[half, lo, u], func=ACT.Relu,
                                     bias=shift[:, half, u : u + 1], scale=gain[:, half, u : u + 1])

        def vector_drain(half, lo, hi, slots):
            first, dst = find(slot_rows, ("h", half), lo, hi)
            for u in slots:
                nc.vector.tensor_scalar(out=dst[:, u, :], in0=d_sums[half, lo, u], scalar1=gain[:, half, u : u + 1],
                                        scalar2=shift[:, half, u : u + 1], op0=ALU.mult, op1=ALU.add)

        def sign_rows(g, slots):
            for s in slots:
                nc.vector.tensor_scalar(out=v_rows[g][:, s, :], in0=v_raw[g][:, s, :], scalar1=sign[:, g, s : s + 1], scalar2=None, op0=ALU.mult)

        def scalar_sign_rows(g, slots):
            for s in slots:
                nc.scalar.activation(out=v_rows[g][:, s, :], in_=v_raw[g][:, s, :], func=ACT.Copy, scale=sign[:, g, s : s + 1])

        def y_banks(lo, hi, banks):
            per = PACK // len(banks)
            for n, number in enumerate(banks):
                tile = bank("y%d_%d" % (lo, n), number, [P, per, BANK // per])
                group = {"columns left": 2 * per * (hi - lo), "open": False}
                for m in range(per):
                    y_sums[n * per + m, lo] = tile[:, m, : hi - lo]
                    y_groups[n * per + m, lo] = group

        def product2(base, lo, hi, g, tiles):
            for q in tiles:
                group = y_groups[q, base]
                group["columns left"] = group["columns left"] - (hi - lo)
                mx_pass(y_sums[q, base][:, lo - base : hi - base], "v", q * P, "h", g, lo, hi,
                        not group["open"], group["columns left"] == 0)
                group["open"] = True

        def finish(lo, hi, tiles=range(N // P)):
            for q in tiles:
                res = sb("y_sb%d_%d" % (q, lo), [P, hi - lo], F32)
                nc.scalar.activation(out=res[:], in_=y_sums[q, lo], func=ACT.Gelu_apprx_tanh, bias=b_sb[:, q : q + 1])
                nc.sync.dma_start(out=out[q * P : (q + 1) * P, lo:hi], in_=res[:])

        cb_sb = sb("cb_sb", [P, 2, PACK], F32)
        b_sb = sb("b_sb", [P, N // P], F32)
        sign = sb("sign", [P, 2, PACK], F32)
        gain = sb("gain", [P, 2, PACK], F32)
        shift = sb("shift", [P, 2, PACK], F32)
        stage = sb("stage", [P, PASS], F32)
        ident = sb("ident", [P, P], F32)

        def load_vectors():
            nc.sync.dma_start(out=stage[CW_ROWS, :], in_=cw.rearrange("(g c) -> g c", g=2))
            nc.sync.dma_start(out=stage[CB_ROWS, :], in_=cb.rearrange("(g c) -> g c", g=2))
            nc.sync.dma_start(out=stage[B_ROWS, 0:P], in_=b.rearrange("(q p) -> q p", p=P))

        def turn_vectors():
            turned = bank("turned", 6, [P, PACK, P])
            turned_b = bank("turned_b", 7, [P, P])
            for slot in range(PACK):
                nc.tensor.transpose(turned[:, slot, :], stage[:, slot::PACK], ident[:])
            nc.tensor.transpose(turned_b[:], stage[:, 0:P], ident[:])
            nc.scalar.activation(out=gain[:], in_=turned[:, :, CW_ROWS].rearrange("p s g -> p g s"), func=ACT.Abs)
            nc.scalar.activation(out=sign[:], in_=turned[:, :, CW_ROWS].rearrange("p s g -> p g s"), func=ACT.Sign)
            nc.scalar.copy(out=cb_sb[:], in_=turned[:, :, CB_ROWS].rearrange("p s g -> p g s"))
            return turned_b

        def derive_constants():
            nc.vector.tensor_tensor(out=shift[:], in0=cb_sb[:], in1=gain[:], op=ALU.mult)

        def warm_table():
            warm = sb("warm", [P, 1], F32)
            nc.scalar.activation(out=warm[:], in_=ident[:, 0:1], func=ACT.Gelu_apprx_tanh)

        def warm_operand():
            words = sb("warm_codes", [P, CHUNK], U32)
            scales = sb("warm_scales", [P, CHUNK], U8)
            nc.vector.quantize_mx(out=words[:].bitcast(FP8X4), scales=scales[:], in_=ones[:])
            return words, scales

        def warm_array(words, scales):
            sink = bank("warm_sink", 7, [P, CHUNK])
            for n in range(WARM_PASSES):
                nc.tensor.matmul_mx(out=sink[:], lhsT=words[:, 0:P].bitcast(FP8X4), lhsT_scale=scales[:, 0:P],
                                    rhs=words[:].bitcast(FP8X4), rhs_scale=scales[:], start=True, stop=True)

        chunks = [(lo, lo + CHUNK) for lo in range(0, T, CHUNK)]
        c0, c1, c2, c3 = chunks
        halves = [(0, PASS), (PASS, J)]
        tiles = [(q * P, (q + 1) * P) for q in range(N // P)]

        nc.vector.memset(stage[:], 0.0)
        make_identity(nc, ident[:])
        load("w", w, 0, 0, J)
        load_vectors()
        load_v(0)
        load("w", w, 1, 0, J)
        for lo, hi in chunks:
            load("x", x, 0, lo, hi)
            load("x", x, 1, lo, hi)
        load_v(1)
        warm_table()
        ones = sb("warm_values", [P, PACK * CHUNK], BF16)
        nc.gpsimd.memset(ones[:], 1.0)
        for lo, hi in chunks:
            operand_tiles("x", lo, hi)
            operand_tiles("h", lo, hi)
            h_row_tiles(lo, hi)
        for lo, hi in halves:
            operand_tiles("w", lo, hi)
        operand_tiles("v", 0, N)
        v_rows[0] = sb("v_rows0", [P, PACK, N], BF16)
        slot_rows["v", 0] = [(0, N, v_rows[0][:])]

        for lo, hi in halves:
            shared_weave("w", 0, lo, hi, W_SHARE)
        turned_b = turn_vectors()
        for lo, hi in halves:
            quantize("w", 0, lo, hi)
        derive_constants()
        scalar_sign_rows(0, [2, 3])
        sign_rows(0, [0, 1])
        weave("v", 0, 0, N)
        quantize("v", 0, 0, N)
        warm_words, warm_scales = warm_operand()

        shared_weave("w", 1, *halves[0], W_SHARE)
        nc.scalar.copy(out=b_sb[:], in_=turned_b[:, B_ROWS])
        warm_array(warm_words, warm_scales)
        shared_weave("w", 1, *halves[1], W_LAST_SHARE)
        weave("x", 0, *c0)
        quantize("w", 1, 0, 2 * P)
        quantize("x", 0, *c0)
        product1(0, *c0, [0, 1, 2, 3], [0])
        shared_weave("x", 1, *c0, X_FIRST_SHARE)
        quantize("w", 1, 2 * P, PASS)
        quantize("x", 1, *c0)
        product1(0, *c0, [0, 1, 2, 3], [1])
        quantize("w", 1, *halves[1])
        product1(1, *c0, [4, 5])

        shared_weave("x", 0, *c1, X_GAP_SHARE)
        vector_drain(0, *c0, [0, 1])
        drain(0, *c0, [2, 3])
        quantize("x", 0, *c1)
        product1(0, *c1, [6, 7], [0])
        weave("x", 1, *c1)
        drain(1, *c0)
        weave("h", 0, *c0)
        quantize("x", 1, *c1)
        product1(0, *c1, [6, 7], [1])
        product1(1, *c1, [0, 1])

        shared_weave("x", 0, *c2, X_THIRD_SHARE)
        drain(0, *c1)
        weave("h", 1, *c0)
        quantize("h", 0, *c0)
        weave("x", 1, *c2)
        quantize("x", 0, *c2)
        product1(0, *c2, [2, 3], [0])
        quantize("x", 1, *c2)
        product1(0, *c2, [2, 3], [1])
        quantize("h", 1, *c0)
        product1(1, *c2, [4, 5])
        drain(1, *c1)

        weave("h", 0, *c1)
        shared_weave("x", 0, *c3, X_LAST_SHARE)
        drain(0, *c2)
        quantize("h", 0, *c1)
        weave("x", 1, *c3)
        quantize("x", 0, *c3)
        product1(0, *c3, [6, 7], [0])
        quantize("x", 1, *c3)
        drain(1, *c2)
        product1(0, *c3, [6, 7], [1])
        product1(1, *c3, [0, 1])
        weave("h", 1, *c1)
        shared_weave("h", 0, *c2, H_THIRD_SHARE)
        drain(0, *c3)

        signed_weave(*tiles[0])
        quantize("h", 1, *c1)
        y_banks(c0[0], c1[1], [2, 3, 4, 5])
        for q, (lo, hi) in enumerate(tiles):
            if q + 1 == len(tiles):
                weave("h", 1, *c2)
            elif q > 0:
                signed_weave(*tiles[q + 1])
            quantize("v", 1, lo, hi)
            if q == 0:
                signed_weave(*tiles[1])
            for g in range(2):
                product2(c0[0], *c0, g, [q])
                product2(c0[0], *c1, g, [q])
        drain(1, *c3, [0, 1])
        finish(c0[0], c1[1], [0])
        drain(1, *c3, [2])
        finish(c0[0], c1[1], [1])
        drain(1, *c3, [3])
        finish(c0[0], c1[1], [2, 3])

        quantize("h", 0, *c2)
        quantize("h", 1, *c2)
        y_banks(*c2, [6, 7])
        for pair in ([0, 1], [2, 3]):
            for g in range(2):
                product2(c2[0], *c2, g, pair)
        weave("h", 0, *c3)
        weave("h", 1, *c3)
        finish(*c2)
        quantize("h", 0, *c3)
        y_banks(*c3, [0, 1, 2, 3])
        product2(c3[0], *c3, 0, [0, 1])
        quantize("h", 1, *c3)
        product2(c3[0], *c3, 1, [0, 1])
        for q in (2, 3):
            for g in range(2):
                product2(c3[0], *c3, g, [q])
        finish(*c3)
